import numpy as np, ml_dtypes
CORES = [25,29,65,69,153,157,193,197]
N = 8
import mx_ref
BF = ml_dtypes.bfloat16
def gentries(a):
    return np.ascontiguousarray(a.reshape(8, 16, -1).transpose(0, 2, 1)).reshape(8, -1)
def gtable(e):
    e = np.asarray(e); return np.ascontiguousarray(e.reshape(8, -1, 16).transpose(0, 2, 1)).reshape(128, -1).astype(np.int32)
def gcols(t, e):
    v = np.concatenate([t.reshape(8, 16, -1, 4), np.zeros((8, 16, 1, 4), BF)], axis=2)
    return np.ascontiguousarray(np.stack([v[g][:, e[g]] for g in range(8)])).reshape(128, -1)
def tile(rs):
    return np.stack(rs, axis=2).reshape(128, -1).astype(BF)
def pick(q, e):
    c = np.concatenate([q[0].reshape(128, -1, 4), np.zeros((128, 1, 4), np.uint8)], axis=1); s = np.concatenate([q[1], np.ones((16, 1), np.uint8)], axis=1)
    return (np.ascontiguousarray(c[:, e].reshape(128, -1)), np.ascontiguousarray(s[:, e]))
def join(*qs):
    return (np.concatenate([q[0] for q in qs], axis=1), np.concatenate([q[1] for q in qs], axis=1))
def put(q, e, v):
    c, s = q[0].reshape(128, -1, 4).copy(), q[1].copy(); c[:, e] = v[0].reshape(128, -1, 4); s[:, e] = v[1]
    return (c.reshape(128, -1), s)
def pk(c, s):
    return (np.ascontiguousarray(c), mx_ref.live(s))
def emit(q):
    return q[0], q[1]
def packed(v, rng):
    q = [mx_ref.quantize(np.ascontiguousarray(v[r])) for r in range(N)]
    return np.stack([a for a, b in q]), np.stack([mx_ref.plane(b, rng) for a, b in q])
def values_of_codes():
    e, c = np.zeros((128, 128, 4), np.float32), np.zeros((128, 2, 4), np.uint8)
    e[np.arange(128), np.arange(128), 0] = 1
    c[:127, :, 0] = np.arange(256).reshape(2, 128).T[:127]
    return mx_ref.matmul(mx_ref.quantize(e.reshape(128, 512).astype(BF)), (c.reshape(128, 8), np.full((16, 2), 127, np.uint8))).T.reshape(-1).astype(np.float64)
CODE_VALUE, SCALE_VALUE = values_of_codes(), 2.0 ** (np.arange(256) - 127.0)
def decode(q):
    return (CODE_VALUE[q[0]].reshape(16, 8, -1, 4) * SCALE_VALUE[q[1]][:, None, :, None] + 0.0).reshape(128, -1).astype(np.float32)
def f(rng, *shape):
    return mx_ref.flush((rng.standard_normal(shape, dtype=np.float32) * np.exp2(rng.integers(-2, 3, shape[:-1] + (1,)))).astype(BF))
def wide(rng, *shape, cols=0):
    v = rng.standard_normal(shape, dtype=np.float32) * np.exp2(rng.integers(-12, 13, shape)).astype(np.float32)
    if cols: v *= np.repeat(np.exp2(rng.integers(-cols, cols + 1, shape[:-2] + (1, shape[-1] // 4))) * (rng.random(shape[:-2] + (1, shape[-1] // 4)) > 0.0625), 4, axis=-1).astype(np.float32)
    return mx_ref.flush(v.astype(BF))
C, K, M, R = 384, 32, 12, 3
BASE = M * np.concatenate([np.arange(K), np.arange(K)])
def matrices(a):
    return a.reshape(8, 16, K // 16, M, M).transpose(0, 2, 1, 3, 4).reshape(8, K, M, M).astype(np.int64)
def stored(m):
    return np.ascontiguousarray(m.reshape(8, K // 16, 16, M, M).transpose(0, 2, 1, 3, 4)).reshape(128, -1)
def numbers_of(rng):
    return {"x": np.array(f(rng, N, 128, 4 * C)), "u": np.array(f(rng, N, 128, 512)), "v": np.array(f(rng, N, 128, 512))}
def nodes(rng):
    return np.stack([gtable(np.stack([rng.permutation(C) for g in range(8)])) for r in range(N)])
def arrows(a):
    a = np.triu(a, 1)
    a = a - a.swapaxes(-1, -2)
    return np.stack([stored(a[r]) for r in range(N)]).astype(np.int32)
def some_arrows(rng):
    return rng.integers(-3, 4, (N, 8, K, M, M)) * (rng.random((N, 8, K, M, M)) < 0.6)
def laid(w, nd):
    w = w.reshape(N, 8, 16, C, 4)
    t = np.zeros_like(w)
    for r in range(N):
        e = gentries(nd[r])
        for g in range(8): t[r, g][:, e[g]] = w[r, g]
    return t.reshape(N, 128, 4 * C).astype(BF)
def weights(rng, still=[], by=1.0):
    w = np.array(f(rng, N, 128, 2048)).reshape(N, 8, 16, 4, 8, 16, 4)
    for i in still:
        w[:, :, i] = 0
        w[:, :, :, :, :, i] = 0
    w = mx_ref.flush((w.astype(np.float32) * np.float32(by)).astype(BF))
    c, s = packed(np.ascontiguousarray(w).reshape(N, 128, 2048), rng)
    return {"wc": c, "ws": s}
def setup_inputs(rng):
    return {**numbers_of(rng), "nd": nodes(rng), "ar": arrows(some_arrows(rng)), **weights(rng)}
def setup_inputs_ties(rng):
    d = numbers_of(rng)
    nd = nodes(rng)
    w = d["x"].reshape(N, 8, 16, C, 4)
    w[:, :, 0] = 0
    w[:, :, 0, :, 0] = rng.integers(1, 4, (N, 8, C)).astype(np.float32).astype(BF)
    u = d["u"].reshape(N, 128, 128, 4)
    u[:, :, ::16] = 0
    o = rng.permutation(N)
    for r in range(N):
        for h in range(0, 128, 16): u[r, h, h, 0] = 0.0 if r == o[0] else -1.0 if r == o[1] else 1.0
    return {"x": laid(w, nd), "u": u.reshape(N, 128, 512), "v": d["v"], "nd": nd, "ar": arrows(some_arrows(rng)), **weights(rng, [0])}
def setup_inputs_near(rng):
    d = numbers_of(rng)
    nd = nodes(rng)
    w = d["x"].astype(np.float32).reshape(N, 8, 16, K, M, 4)
    w[:, :, 0] = 0
    w[:, :, 8:] = 0
    s = rng.integers(0, 16, (N, 8, K, M))
    w[:, :, 8] = ((s[..., None] >> np.arange(4)) & 1) * np.exp2(np.arange(4) - 23.0)
    u = d["u"].reshape(N, 128, 128, 4)
    u[:, :, ::16] = 0
    o = rng.permutation(N) % 4
    for r in range(N):
        k = 1.0 if o[r] == 0 else 2.0 ** -30
        c = rng.choice([-1.0, 1.0], (8, K, 1))
        if o[r] < 2:
            w[r, :, 0, :, :, 0] = c
            w[r, :, 11, :, :, 0] = 2.0 ** -10
        elif o[r] == 2:
            far = np.argsort(rng.random((8, K, M)), axis=2)
            w[r, :, 0, :, :, 0] = 1.0 * (far == 0) - 1.0 * (far == 1)
            for g in rng.permutation(8)[:4]: w[r, g, 0, rng.integers(K), rng.integers(M), 0] = 2.0 ** 26
        else:
            w[r, :, 8] = 0
            w[r, :, 8, :, :, 0] = c * rng.integers(8, 16, (8, K, M)) * 2.0 ** -27
        for h in range(0, 128, 16):
            if o[r] < 2:
                u[r, h, h, 0] = k
                u[r, h + 11, h, 0] = k
            if o[r] == 2: u[r, h, h, 0] = 16.0
            if o[r] < 3: u[r, h + 8, h] = k
            else: u[r, h + 8, h, 0] = k
    return {"x": laid(w, nd), "u": u.reshape(N, 128, 512), "v": d["v"], "nd": nd, "ar": arrows(some_arrows(rng)), **weights(rng, [0, 8, 9, 10, 11, 12, 13, 14, 15])}
def setup_inputs_huge(rng):
    d = numbers_of(rng)
    o = rng.permutation(N)
    a = some_arrows(rng)
    x = 0.8 + 0.1 * rng.random((N, 128, C, 4))
    u = d["u"].reshape(N, 128, 128, 4)
    for r in range(N):
        c = rng.choice([-1.0, 1.0], (C, 1))
        k = 2.0 ** 30 * (1.0 - 0.1 * rng.random((128, 8, 4)))
        if o[r] < 2: c = -np.ones((C, 1))
        if o[r] == 3:
            c = -np.ones((C, 1))
            c[rng.permutation(C)[:K]] = 1.0
            x[r] = 0.9375
            k[:] = 2.0 ** 30
        if o[r] % 2 == 1: a[r] = 0
        x[r] *= c * (2.0 ** 30 if o[r] % 2 == 1 else 2.0 ** 28 if o[r] == 0 else 2.0 ** 27)
        u[r, :, ::16] = k.astype(np.float32).astype(BF)
    return {"x": x.astype(np.float32).reshape(N, 128, 4 * C).astype(BF), "u": u.reshape(N, 128, 512), "v": d["v"], "nd": nodes(rng), "ar": arrows(a), **weights(rng, [], 2.0 ** -14)}
def setup_inputs_knots(rng):
    d = numbers_of(rng)
    e = rng.permutation(N)
    kind = rng.integers(0, 4, (N, 8, K, 1, 1))
    kind[e[0]] = 0
    kind[e[1]] = 1
    sign = rng.choice([-1, 1], (N, 8, K, M, M))
    half = sign * (rng.random((N, 8, K, M, M)) < 0.5)
    a = np.where(kind == 0, 0, np.where(kind == 1, sign * rng.integers(1, 4, (N, 8, K, M, M)), np.where(kind == 2, half, 3 * half)))
    place = np.arange(8)[:, None, None] * 4 + np.arange(4)
    most = place == rng.integers(0, 32, (N, 16, 1, C, 1))
    x = (129.0 + 2.0 * rng.integers(0, 64, (N, 16, 8, C, 4))) * np.exp2(-7.0 - rng.integers(8, 15, (N, 16, 8, C, 4)))
    x = np.where(most, 1.96875, x) * rng.choice([-1.0, 1.0], (N, 16, 8, C, 4)) * np.exp2(rng.integers(-2, 3, (N, 16, 1, C, 1)))
    return {"x": x.astype(np.float32).reshape(N, 128, 4 * C).astype(BF), "u": d["u"], "v": d["v"], "nd": nodes(rng), "ar": arrows(a), **weights(rng)}
def setup_inputs_spread(rng):
    d = setup_inputs(rng)
    d["x"] = wide(rng, N, 128, 4 * C, cols=6)
    return d
def check_inputs(d):
    b = []
    for k in ("x", "u", "v"):
        a = np.abs(d[k].astype(np.float32))
        if not (np.isfinite(a).all() and ((a == 0) | (a >= 2.0 ** -30) & (a <= 2.0 ** 30)).all()): b.append("a value of " + k)
    none, least, most = [emit(mx_ref.quantize(np.full((128, 16), k, np.float32).astype(BF)))[1][0, 0] for k in (0.0, 2.0 ** -30, 2.0 ** 30)]
    for r in range(N):
        if (np.sort(gentries(d["nd"][r]), axis=1) != np.arange(C)).any(): b.append("nd: a group without every column once")
        a = matrices(d["ar"][r])
        if (np.abs(a) > 3).any(): b.append("an entry of ar")
        if (a != -a.swapaxes(-1, -2)).any(): b.append("ar: B[j, i] isn't -B[i, j]")
        if ((d["wc"][r] & 0x7F) == 0x7F).any(): b.append("wc: a code that is no number")
        s = mx_ref.live(d["ws"][r])
        if ((s != none) & ((s < least) | (s > most))).any(): b.append("ws: a scale out of range")
    return b
def parts(t, n, e):
    return gcols(t, np.where(e < 0, -1, np.take_along_axis(n, BASE + np.maximum(e, 0), axis=1))).astype(np.float32)
def pair(t, n, w):
    e = np.argsort(-w, axis=2, kind="stable")[:, :, :2]
    e = np.where(np.take_along_axis(w, e, axis=2) > 0, e, -1)
    return ((parts(t, n, e[:, :, 0]) + parts(t, n, e[:, :, 1])) * np.float32(0.5)).astype(BF).astype(np.float32)
def reference(x, u, v, nd, ar, wc, ws):
    qu = [mx_ref.quantize(u[r]) for r in range(N)]
    lay = [pk(wc[r], ws[r]) for r in range(N)]
    now = [x[r] for r in range(N)]
    node = [gentries(nd[r]) for r in range(N)]
    arrow = [matrices(ar[r]) for r in range(N)]
    for t in range(R):
        held, made, sent, into = [], [], [], []
        for r in range(N):
            q = mx_ref.quantize(now[r])
            own = decode(q).astype(BF)
            s = mx_ref.matmul(qu[r], q)[::16] + np.float32(0.0)
            s = np.take_along_axis(s, node[r], axis=1).reshape(8, K, M)
            first = np.argmax(s, axis=2)
            row = np.take_along_axis(arrow[r], first[:, :, None, None], axis=2)[:, :, 0]
            free = (row == 0) & (np.arange(M) != first[:, :, None])
            second = np.argmax(np.where(free, s, -np.inf), axis=2)
            k = np.concatenate([first, second], axis=1)
            full = np.concatenate([np.ones((8, K), bool), free.any(axis=2)], axis=1)
            row = np.concatenate([row, np.take_along_axis(arrow[r], second[:, :, None, None], axis=2)[:, :, 0]], axis=1) * full[:, :, None]
            y = (np.maximum(pair(own, node[r], -row), pair(own, node[r], row)) - parts(own, node[r], np.where(full, k, -1))).astype(BF)
            held.append(own)
            made.append(y)
            sent.append(mx_ref.quantize(y))
            e = np.tile(np.arange(C), (8, 1))
            g, i = np.nonzero(full)
            e[g, np.take_along_axis(node[r], BASE + k, axis=1)[g, i]] = C + i
            into.append(e)
            more = (np.abs(row)[:, :, :, None] * row[:, :, None, :] - row[:, :, :, None] * np.abs(row)[:, :, None, :]) // 2
            turn = np.ones((8, 2 * K, M), np.int64)
            np.put_along_axis(turn, k[:, :, None], np.where(full, -1, 1)[:, :, None], axis=2)
            turn = turn[:, :K] * turn[:, K:]
            arrow[r] = np.clip(arrow[r] + more[:, :K] + more[:, K:], -3, 3) * turn[:, :, :, None] * turn[:, :, None, :]
        for r in range(N):
            q = sent[(r - 1) % N]
            new = tile([mx_ref.matmul(pick(lay[r], np.arange(128 * b, 128 * b + 128)), q) * np.float32(0.03125) + made[r][:, b::4].astype(np.float32) for b in range(4)])
            now[r] = gcols(np.concatenate([held[r], new], axis=1), into[r])
    y, oa = np.zeros((N, 128, C), np.float32), np.zeros(ar.shape, np.float32)
    oc, osc = np.zeros((N, 128, 4 * C), np.uint8), np.zeros((N, 16, C), np.uint8)
    for r in range(N):
        q = mx_ref.quantize(now[r])
        y[r] = mx_ref.matmul(mx_ref.quantize(v[r]), q)
        oa[r] = stored(arrow[r])
        oc[r], osc[r] = emit(q)
    return {"y": y, "oa": oa, "oc": oc, "osc": osc}

@@ -1,0 +1,491 @@
+from concourse.mybir import dt, AluOpType, ActivationFunctionType
+
+N, C, R = 8, 384, 3
+BIG = 2.0 ** 90
+PEN, NONE = 2.0 ** 80, 2.0 ** 79
+Q = 8192.0
+CW = 416
+SCRATCH, CODES = {}, set()
+
+
+def declare(dtype, spec):
+    for item in spec.split():
+        name, cols = item.split(":")
+        where = "psum" if name in ("psP", "psE") else "sbuf"
+        SCRATCH[name] = (where, [128, int(cols)], dtype)
+        if dtype == "float8_e4m3fn_x4":
+            CODES.add(name)
+
+
+declare("bfloat16", "fx:1664 fh:1664 ut:512 vt0:512 yt:512 zt:512 et:520 ones:128 ga:512 gk:256 gs:512 gm2:256 y32:256 vt:256 "
+        "h1:364 h2:364 pw:144 w:104 pp:52 nn:52 oo:52 ei:576 pr:576 s5:576 sp:144 iC:384 cap:384 we:182 rs2:384 sg:576")
+declare("float8_e4m3fn_x4", "uq:128 urq:128 vq:128 eq:512 zq:128 wq:512 xq:384 " + " ".join("yc%d:128 lc%d:128 rc%d:64" % (t, t, t) for t in range(R)))
+declare("uint8", "us:128 urs:128 vs:128 es:512 zs:128 wp:512 xs:384 " + " ".join("yp%d:128 lp%d:128 rp%d:64" % (t, t, t) for t in range(R)))
+declare("float32", "psP:1536 psE:2048 vf:256 psc:384 gm:384 sc:384 pm1:24 ix:4 junk:64 s2:364 pm2:26 kk:728 ka:104 pmb:105 mn:104 sm:104 "
+        "bt:368 pen:368 win1:344 win2:344 tb1:368 tp0:368 ob:288 ysb:384 rt:384 nlf:24 iK:384 pf:4 pd:8 it13:13 k2i:24 k2c:52 cli:24 "
+        "rsx:160 lm:46 lA:46 lB:46 lC:46 lD:46 lE:46 lF:46 lG:46 lH:46 lI:46 uA:36 uX:36 uY:36 uZ:36 uB:36 uC:36")
+declare("int32", "di:16 dj:16 ndi:24 ari:288 pI:4 pA:4 ui:8 li:46")
+declare("uint16", "oL:20 so:16 nd16:24 nl:24 cl:24 ul:8 L:156")
+PART = {"oA": ("oL", 0, 8), "oB": ("oL", 8, 8), "oK": ("oL", 16, 4), "rs24": ("rsx", 0, 24), "rs26": ("rsx", 24, 26), "rsk": ("rsx", 52, 104),
+        "LI": ("L", 48, 36), "LJ": ("L", 84, 36), "L4": ("L", 120, 36)}
+DMAS = 24
+SEMAPHORES = ["qv", "qs", "qt", "qg", "sent"] + ["d%d" % i for i in range(DMAS)] + ["ac%d" % t for t in range(R)] + ["ap%d" % t for t in range(R)]
+
+
+def route(T, topo, r):
+    src, dst = T.cores[r], T.cores[(r + 1) % N]
+    if topo.may_write(src, dst):
+        return src, dst, None, None
+    c = [k for k in topo.cores_of(src) if k not in T.cores and topo.may_write(k, dst)]
+    c.sort(key=lambda k: (topo.die(k) != topo.die(src), k))
+    return src, dst, c[0], c[1 % len(c)]
+
+
+def u8(T, name, a, b):
+    v = T[name][:, a:b]
+    return v.bitcast(dt.uint8) if name in CODES else v
+
+
+def send(g, T, topo, core, to, out, src, sem):
+    rid, pid = topo.addr(to, core)
+    g.remote_dma(u8(T, out, 0, 64), u8(T, src, 0, 64), T.sem[sem], T.sem.sent, pid, rid, topo.mask(core, to))
+    return len(topo.engines(core, to))
+
+
+def relay_program(g, core, T, topo):
+    total = 0
+    for t in range(R):
+        for r in range(N):
+            src, dst, ca, cb = route(T, topo, r)
+            for k, sem, mid, out in ((ca, "ac%d" % t, "rc%d" % t, "lc%d" % t), (cb, "ap%d" % t, "rp%d" % t, "lp%d" % t)):
+                if k == core:
+                    g.wait_ge(T.sem[sem], len(topo.engines(src, core)))
+                    total += send(g, T, topo, core, dst, out, mid, sem)
+    if total:
+        g.wait_ge(T.sem.sent, total)
+
+
+def overlap(a, b):
+    if a[0] != b[0] or a[1] >= b[2] or b[1] >= a[2]:
+        return False
+    return not (a[3] == b[3] > 1 and (a[1] - b[1]) % a[3])
+
+
+def rank_program(g, core, T, topo):
+    rank = T.rank_of(core)
+    if rank is None:
+        relay_program(g, core, T, topo)
+        return
+    A = AluOpType
+    F = ActivationFunctionType
+    queue = {"v": g.vector, "s": g.scalar, "t": g.tensor, "g": g, "y": g.sync}
+    count = {}
+    known = {k: {} for k in queue}
+    log = {}
+    free = ["d%d" % i for i in range(DMAS)]
+
+    def need(q, sem, val, clock):
+        if known[q].get(sem, 0) < val:
+            queue[q].wait_ge(T.sem[sem], val)
+            known[q][sem] = val
+            for s in clock:
+                known[q][s] = max(known[q].get(s, 0), clock[s])
+
+    def waits(q, reads, writes):
+        w = []
+        for kind, regions in (("r", reads), ("w", writes)):
+            for x in regions:
+                for k, y, sem, val, clock in log.get(x[0], []):
+                    if (kind == "w" or k == "w") and overlap(x, y):
+                        w.append((sem, val, clock))
+        w.sort(key=lambda e: -e[1])
+        for sem, val, clock in w:
+            need(q, sem, val, clock)
+
+    def note(q, reads, writes, sem, val):
+        clock = dict(known[q])
+        for x in writes:
+            log[x[0]] = [e for e in log.get(x[0], []) if not (e[1][1] >= x[1] and e[1][2] <= x[2] and x[3] == 1)]
+        for kind, regions in (("r", reads), ("w", writes)):
+            for x in regions:
+                log.setdefault(x[0], []).append((kind, x, sem, val, clock))
+
+    def run(q, call, reads, writes):
+        reads = [x for o in reads for x in o[1]]
+        writes = [x for o in writes for x in o[1]]
+        both = [x for x in reads if x[0] in ("psP", "psE")]
+        reads = [x for x in reads if x not in both]
+        waits(q, reads + both, writes + both)
+        sem = "q" + q
+        count[sem] = count.get(sem, 0) + 1
+        call(queue[q]).then_inc(T.sem[sem], 1)
+        note(q, reads, writes + both, sem, count[sem])
+
+    def dma(q, out, in_, reads, writes):
+        waits(q, reads, writes)
+        sem = free.pop(0)
+        count[sem] = 16
+        queue[q].dma_start(out, in_).then_inc(T.sem[sem], 16)
+        note(q, reads, writes, sem, 16)
+
+    def V(name, a=0, b=None, step=1):
+        name, o, n = PART.get(name, (name, 0, None))
+        b = (SCRATCH[name][1][1] if n is None else n) if b is None else b
+        a, b = a + o, b + o
+        return (T[name][:, a:b:step] if step > 1 else T[name][:, a:b], [(name, a, b, step)])
+
+    def ind(win, off):
+        return (win[0].indirect(off[0]), win[1] + off[1])
+
+    def val(s):
+        return s[0] if isinstance(s, tuple) else s
+
+    def reg(*ss):
+        return [s for s in ss if isinstance(s, tuple)]
+
+    def tt(out, a, b, op):
+        run("v", lambda e: e.tensor_tensor(out[0], a[0], b[0], op), [a, b], [out])
+
+    def ts(out, a, s1, op0, s2=None, op1=None):
+        if op1 is None:
+            run("v", lambda e: e.tensor_scalar(out[0], a[0], val(s1), None, op0), [a] + reg(s1), [out])
+        else:
+            run("v", lambda e: e.tensor_scalar(out[0], a[0], val(s1), val(s2), op0, op1), [a] + reg(s1, s2), [out])
+
+    def cp(out, a):
+        run("v", lambda e: e.tensor_copy(out[0], a[0]), [a], [out])
+
+    def scan(out, d0, d1, initial, op0, op1):
+        run("v", lambda e: e.tensor_tensor_scan(out[0], d0[0], d1[0], initial, op0, op1), [d0, d1], [out])
+
+    def fill(out, c):
+        run("v", lambda e: e.memset(out[0], c), [], [out])
+
+    def quant(q, s, t):
+        run("v", lambda e: e.quantize_mx(q[0], s[0], t[0]), [t], [q, s])
+
+    def mm(out, w, ws, x, xs):
+        run("t", lambda e: e.matmul_mx(out[0], w[0], ws[0], x[0], xs[0], True, True), [w, ws, x, xs], [out])
+
+    def act(out, a, scale=1.0, func=None, bias=None, accum=None):
+        kw = {}
+        if scale != 1.0:
+            kw["scale"] = scale
+        if bias is not None:
+            kw["bias"] = val(bias)
+            func = func or F.Identity
+        if accum is not None:
+            kw["accum_out"] = accum[0]
+        run("s", lambda e: e.activation(out[0], a[0], func or F.Copy, **kw), [a] + reg(bias), [out] + reg(accum))
+
+    def iota(out, pattern, base=0, cm=0):
+        if SCRATCH[out[1][0][0]][2] == "int32":
+            run("g", lambda e: e.iota(out[0], pattern, base, cm), [], [out])
+        else:
+            run("g", lambda e: e.iota(out[0], pattern, base, cm, allow_small_or_imprecise_dtypes=True), [], [out])
+
+    def select(out, pattern, fill_, base):
+        run("g", lambda e: e.affine_select(out[0], out[0], pattern, A.not_equal, fill_, base, 0), [out], [out])
+
+    dma("y", T.ndi[:], T.nd[:], [], V("ndi")[1])
+    dma("s", T.ut[:], T.u[:], [], V("ut")[1])
+    dma("y", T.fx[:, 0:768], T.x[:, 0:768], [], V("fx", 0, 768)[1])
+    dma("s", T.fx[:, 768:1536], T.x[:, 768:1536], [], V("fx", 768, 1536)[1])
+    dma("y", T.ari[:], T.ar[:], [], V("ari")[1])
+    dma("y", T.wq[:, 0:512].bitcast(dt.uint8), T.wc[:], [], V("wq")[1])
+    dma("y", T.wp[:], T.ws[:], [], V("wp")[1])
+    dma("y", T.vt0[:], T.v[:], [], V("vt0")[1])
+
+    lm = lambda n, a=0, b=46: V(n, a, b)
+    fill(V("ones"), 1.0)
+    fill(V("et"), 0.0)
+    fill(V("rsx"), BIG)
+    iota(V("pI"), [[0, 4]], 0, 1)
+    iota(lm("lm"), [[0, 2], [16, 23]])
+    iota(V("cli"), [[192, 2], [1, 12]])
+    iota(V("uA"), [[0, 2], [1, 6], [4, 3]], 1)
+    iota(V("uZ"), [[144, 2], [0, 6], [48, 3]])
+    iota(V("iK"), [[1, 384]])
+    iota(V("iC"), [[0, 24], [1, 16]])
+    iota(V("ui"), [[16, 8]])
+    run("g", lambda e: e.affine_select(T.et[:, 3:515:4], T.ones[:], [[-1, 128]], A.is_equal, 0.0, 0, 1), [V("ones")], [V("et")])
+    iota(V("k2i"), [[0, 2], [-512, 12]], -512)
+    for n in ("win1", "win2"):
+        iota(V(n, 288, 344), [[0, 56]])
+    for k, c in ((1, PEN), (39, NONE), (53, NONE)):
+        select(V("win2", 288, 344), [[1, 56]], c, -k)
+    select(V("rs24"), [[0, 2], [1, 12]], -BIG, 0)
+    select(V("rs26"), [[0, 2], [1, 13]], -BIG, 0)
+    iota(V("we"), [[0, 13], [1, 14]])
+    iota(V("k2c"), [[0, 52]], -8192)
+    select(V("rsk"), [[0, 8], [1, 13]], -BIG, -12)
+    for b in range(4):
+        iota(V("fh", CW * b + 384, CW * b + CW), [[0, 32]])
+    iota(V("yt", 256, 512), [[0, 256]])
+    iota(V("uX"), [[13, 2], [0, 18]])
+    iota(V("uY"), [[13, 2], [0, 6], [4, 3]])
+    iota(V("it13"), [[1, 13]])
+    iota(V("zt"), [[0, 512]])
+
+    ts(V("pA", 0, 1), V("pI", 0, 1), 15, A.bitwise_and)
+    ts(V("pA", 1, 2), V("pI", 1, 2), 2, A.logical_shift_right, 3, A.bitwise_and)
+    ts(V("pA", 2, 3), V("pI", 2, 3), 3, A.bitwise_and)
+    ts(V("pA", 3, 4), V("pI", 3, 4), 1, A.bitwise_and)
+    cp(V("pf"), V("pA"))
+    p16, p4, pt, p1 = (V("pf", k, k + 1) for k in range(4))
+    act(V("pd", 2, 3), p16, -1.0, bias=182.0)
+    act(V("pd", 0, 1), p16, 12.0)
+    act(V("pd", 5, 6), p4, 12.0)
+    act(V("uB"), V("uA"), bias=p4)
+    ts(lm("lB"), lm("lm"), V("pd", 2, 3), A.is_ge)
+    ts(V("cl"), V("cli"), V("pd", 0, 1), A.add)
+    ts(lm("lC"), lm("lB"), -182.0, A.mult, p16, A.add)
+    ts(V("uC"), V("uB"), 12.0, A.is_ge, -12.0, A.mult)
+    tt(lm("lD"), lm("lC"), lm("lm"), A.add)
+    tt(V("uC"), V("uC"), V("uB"), A.add)
+    ts(lm("li"), lm("lD"), 1.0 / 14, A.mult, -6.5 / 14, A.add)
+    fill(V("pmb", 0, 1), -BIG)
+    cp(lm("lE"), lm("li"))
+    tt(V("uZ"), V("uZ"), V("uC"), A.add)
+    ts(lm("lC"), lm("lE"), -14.0, A.mult)
+    ts(V("L4"), V("uZ"), V("pd", 5, 6), A.add)
+    tt(lm("lF"), lm("lC"), lm("lD"), A.add)
+    ts(lm("lF", 23, 46), lm("lF", 23, 46), 1.0, A.add)
+    tt(lm("lC"), lm("lF"), lm("lE"), A.subtract)
+    act(lm("lI"), lm("lB"), 72.0)
+    ts(lm("lD"), lm("lC"), 0.0, A.is_lt, 12.0, A.mult)
+    tt(lm("lC"), lm("lC"), lm("lD"), A.add)
+
+    def score_products(w, ws):
+        for k in range(3):
+            a = 128 * k
+            quant(V("xq", a, a + 128), V("xs", a, a + 128), V("fx", 4 * a, 4 * a + 512))
+            mm(V("psP", 512 * k, 512 * k + 128), w, ws, V("xq", a, a + 128), V("xs", a, a + 128))
+
+    def unpack_products():
+        for b in range(4):
+            mm(V("psE", 512 * b, 512 * b + 384), V("eq", 128 * b, 128 * b + 128), V("es", 128 * b, 128 * b + 128), V("xq"), V("xs"))
+
+    cp(V("nd16"), V("ndi"))
+    act(V("rt"), ind(V("iK"), V("nd16")))
+    act(V("cap"), V("iC"), -1.0, F.Square, p16)
+    act(V("cap"), V("cap"), -2.0 * BIG, bias=BIG)
+    fill(V("rs2"), BIG)
+    cp(V("ul"), V("ui"))
+    fill(V("rs2", 0, 384, 16), -BIG)
+    quant(V("uq"), V("us"), V("ut"))
+    run("v", lambda e: e.tensor_copy(T.urq[:, 0:128].bitcast(dt.uint32), T.uq[:, 0:128].bitcast(dt.uint32).indirect(T.ul[:, 0:8])), [V("uq"), V("ul")], [V("urq")])
+    act(V("urs"), ind(V("us"), V("ul")))
+    score_products(V("urq"), V("urs"))
+    tt(V("gm"), ind(V("rt"), V("cl")), V("cap"), A.min)
+    act(V("ei"), ind(V("ari"), V("L4")))
+    scan(V("sc"), V("rs2"), V("gm"), -BIG, A.min, A.max)
+    act(V("pw"), V("ei", 0, 576, 4))
+    cp(V("nl"), V("sc", 15, 384, 16))
+    act(V("nlf"), V("sc", 15, 384, 16))
+    act(lm("lG"), lm("lC"), 12.0, bias=-12.0)
+    act(lm("lD"), lm("lC"), -12.0, bias=276.0)
+    ts(lm("lH"), lm("lC"), 7.0, A.is_ge, 1000.0, A.mult)
+    tt(lm("lG"), lm("lG"), lm("lE"), A.add)
+    tt(lm("lD"), lm("lD"), lm("lF"), A.add)
+    tt(lm("lG"), lm("lG"), lm("lH"), A.add)
+    ts(lm("lH"), lm("lC"), 0.0, A.is_equal, 289.0, A.mult)
+    tt(lm("lG"), lm("lG"), lm("lD"), A.min)
+    tt(lm("lG"), lm("lG"), lm("lI"), A.add)
+    tt(lm("lG"), lm("lG"), lm("lH"), A.max)
+    e0, e1 = lm("lF", 0, 23), lm("lF", 23, 46)
+    act(lm("lA"), lm("lB"), 14.0, bias=314.0)
+    act(lm("lC", 0, 23), lm("lB", 0, 23), 12.0, bias=290.0)
+    ts(lm("lH"), lm("lF"), 12.0, A.is_ge, 288.0, A.mult)
+    ts(lm("lI"), lm("lE"), 12.0, A.is_equal)
+    tt(lm("lG"), lm("lG"), lm("lH"), A.max)
+    tt(lm("lA"), lm("lA"), lm("lF"), A.add)
+    tt(lm("lC", 0, 23), lm("lC", 0, 23), lm("lE", 0, 23), A.add)
+    ts(lm("lD", 0, 23), e0, 13.0, A.is_equal)
+    ts(lm("lD", 23, 46), e1, 13.0, A.is_lt)
+    tt(lm("lA"), lm("lA"), lm("lI"), A.mult)
+    tt(lm("lC", 0, 23), lm("lC", 0, 23), lm("lD", 0, 23), A.mult)
+    tt(lm("lA", 23, 46), lm("lA", 23, 46), lm("lD", 23, 46), A.mult)
+    tt(lm("lG", 0, 23), lm("lG", 0, 23), lm("lC", 0, 23), A.max)
+    tt(lm("lG"), lm("lG"), lm("lA"), A.max)
+    cp(V("L", 0, 23), lm("lG", 0, 23))
+    cp(V("L", 24, 47), lm("lG", 23, 46))
+    L0, L1 = V("L", 0, 23), V("L", 24, 47)
+
+    def penalties():
+        act(V("win2", 0, 144), V("pw"), PEN, F.Abs)
+        act(V("win2", 144, 288), V("pw"), PEN, F.Abs)
+        act(V("tp0"), ind(V("win2"), L0))
+
+    def weights():
+        act(V("win1", 0, 144), V("pw"), Q)
+        act(V("win1", 144, 288), V("pw"), -Q)
+        act(V("tb1"), ind(V("win1"), L1))
+
+    def table_p():
+        tt(V("pen"), ind(V("win2"), L1), V("tp0"), A.subtract)
+
+    def table_b():
+        tt(V("bt"), ind(V("win1"), L0), V("tb1"), A.subtract)
+
+    direct = route(T, topo, (rank - 1) % N)[2] is None
+    late = True
+    for t in range(R):
+        if t:
+            score_products(V("urq"), V("urs"))
+            unpack_products()
+        for k in range(3):
+            (cp if t else act)(V("psc", 128 * k, 128 * k + 128), V("psP", 512 * k, 512 * k + 128))
+
+        def unpack(b):
+            act(V("fh", CW * b, CW * b + 384), V("psE", 512 * b, 512 * b + 384), 0.5)
+
+        def which(src, n, k):
+            for x in range(2):
+                end = n * x + n - 1
+                act(V("junk", 16 * (k + x), 16 * (k + x) + n), V(src, n * x, end + 1), -1.0, F.Sign, V(src, end, end + 1), V("ix", k + x, k + x + 1))
+
+        if t:
+            unpack(0)
+            unpack(1)
+        tt(V("gm"), ind(V("psc"), V("nl")), V("cap"), A.min)
+        if t == 0:
+            tt(V("win1", 290, 314), V("nlf"), V("k2i"), A.add)
+            penalties()
+        scan(V("sc"), V("rs2"), V("gm"), -BIG, A.min, A.max)
+        scan(V("pm1"), V("rs24"), V("sc", 15, 384, 16), -BIG, A.min, A.max)
+        which("pm1", 12, 0)
+        if late:
+            table_p()
+        for x in range(2):
+            cp(V("pen", 182 * x + 13, 182 * x + 13 + 155, 14), V("sc", 192 * x + 15, 192 * x + 192, 16))
+        if t:
+            unpack(2)
+            unpack(3)
+        else:
+            for x in range(2):
+                act(V("win1", 314 + 14 * x, 326 + 14 * x), V("nlf", 12 * x, 12 * x + 12), bias=-4096.0)
+                act(V("win1", 326 + 14 * x, 327 + 14 * x), p16, bias=384.0 + 16 * x - 4096.0)
+            weights()
+            for x in range(4):
+                act(V("k2c", 13 * x, 13 * x + 12), V("win1", 290 + 12 * (x % 2), 302 + 12 * (x % 2)))
+            for b in range(4):
+                quant(V("eq", 128 * b, 128 * b + 128), V("es", 128 * b, 128 * b + 128), V("et", 3 - b, 515 - b))
+            unpack_products()
+        for x in range(2):
+            ts(V("h1", 182 * x, 182 * x + 182), V("we"), V("ix", x, x + 1), A.is_gt)
+        scan(V("s2"), V("h1"), V("pen", 0, 364), 0.0, A.mult, A.add)
+        scan(V("pm2"), V("rs26"), V("s2", 13, 364, 14), -BIG, A.min, A.max)
+        which("pm2", 13, 2)
+        if late:
+            table_b()
+        if t == 0:
+            for b in range(4):
+                unpack(b)
+        scan(V("kk", 0, 364), V("h1"), V("bt", 0, 364), 0.0, A.mult, A.add)
+        for x in range(2):
+            ts(V("h2", 182 * x, 182 * x + 182), V("we"), V("ix", 2 + x, 3 + x), A.is_gt)
+        scan(V("kk", 364, 728), V("h2"), V("bt", 0, 364), 0.0, A.mult, A.add)
+        tt(V("ka", 52, 104), V("k2c"), V("kk", 12, 728, 14), A.subtract)
+        cp(V("ka", 0, 52), V("kk", 13, 728, 14))
+        ts(V("oK"), V("kk", 181, 728, 182), 4096.0, A.add)
+        for b in range(4):
+            act(V("gk", 64 * b, 64 * b + 64), ind(V("fh", CW * b, CW * b + CW), V("oK")), 2.0)
+        scan(V("pmb", 1, 105), V("rsk"), V("ka"), -BIG, A.min, A.max)
+        ts(V("di", 0, 8), V("pmb", 12, 105, 13), 384.0, A.max)
+        tt(V("mn"), V("ka"), V("pmb", 0, 104), A.min)
+        ts(V("dj", 0, 8), V("di", 0, 8), 511, A.bitwise_and)
+        scan(V("sm"), V("rsk"), V("mn"), -BIG, A.min, A.max)
+        cp(V("oA"), V("dj", 0, 8))
+        for b in range(4):
+            act(V("ga", 128 * b, 128 * b + 128), ind(V("fh", CW * b, CW * b + CW), V("oA")))
+        ts(V("di", 8, 16), V("sm", 11, 104, 13), 384.0, A.max)
+        ts(V("dj", 8, 16), V("di", 8, 16), 511, A.bitwise_and)
+        cp(V("oB"), V("dj", 8, 16))
+        for b in range(4):
+            tt(V("gs", 128 * b, 128 * b + 128), ind(V("fh", CW * b, CW * b + CW), V("oB")), V("ga", 128 * b, 128 * b + 128), A.add)
+            if b:
+                tt(V("gm2", 64 * b - 64, 64 * b), V("gs", 128 * b - 128, 128 * b - 64), V("gs", 128 * b - 64, 128 * b), A.max)
+        tt(V("yt", 0, 256, 4), V("gm2", 0, 64), V("gk", 0, 64), A.subtract)
+        tt(V("gm2", 192, 256), V("gs", 384, 448), V("gs", 448, 512), A.max)
+        for b in range(1, 4):
+            tt(V("yt", b, 256, 4), V("gm2", 64 * b, 64 * b + 64), V("gk", 64 * b, 64 * b + 64), A.subtract)
+        quant(V("yc%d" % t), V("yp%d" % t), V("yt"))
+        waits("g", [("yc%d" % t, 0, 128, 1), ("yp%d" % t, 0, 128, 1)], [])
+        src, dst, ca, cb = route(T, topo, rank)
+        for k, sem, mid, out, mine in ((ca, "ac%d" % t, "rc%d" % t, "lc%d" % t, "yc%d" % t), (cb, "ap%d" % t, "rp%d" % t, "lp%d" % t, "yp%d" % t)):
+            count["sent"] = count.get("sent", 0) + send(g, T, topo, core, dst if k is None else k, out if k is None else mid, mine, sem)
+        for f in range(2):
+            for x in range(2):
+                ts(V("oo", 26 * f + 13 * x, 26 * f + 13 * x + 13), V("it13"), V("ix", 2 * f + x, 2 * f + x + 1), A.is_equal, -2.0, A.mult)
+        ts(V("pp"), V("kk", 12, 728, 14), -1.0 / Q, A.mult, 0.0, A.max)
+        ts(V("nn"), V("kk", 12, 728, 14), 1.0 / Q, A.mult, 0.0, A.max)
+        if t == 0:
+            ts(V("pd", 3, 4), pt, 26.0, A.mult, p4, A.add)
+            ts(V("pd", 4, 5), p1, -52.0, A.mult, 26.0, A.add)
+            tt(V("uX"), V("uX"), V("uC"), A.add)
+            ts(V("pd", 6, 7), pt, 26.0, A.mult, V("pd", 4, 5), A.add)
+            ts(V("LI"), V("uY"), V("pd", 3, 4), A.add)
+            ts(V("LJ"), V("uX"), V("pd", 6, 7), A.add)
+        tt(V("w", 26, 78), V("pp"), V("oo"), A.add)
+        for f in range(2):
+            tt(V("w", 78 * f, 78 * f + 26), V("nn", 26 * f, 26 * f + 26), V("oo", 26 * f, 26 * f + 26), A.add)
+        if t == 0:
+            fill(V("sg"), -1.0)
+            quant(V("zq"), V("zs"), V("zt"))
+            fill(V("sg", 0, 576, 4), 0.0)
+            fill(V("sg", 2, 576, 4), 1.0)
+            for k in range(R):
+                dma("y", u8(T, "lc%d" % k, 64, 128), u8(T, "zq", 64, 128), V("zq")[1], V("lc%d" % k, 64, 128)[1])
+                dma("y", u8(T, "lp%d" % k, 64, 128), u8(T, "zs", 64, 128), V("zs")[1], V("lp%d" % k, 64, 128)[1])
+        for b in range(4):
+            act(V("y32", 64 * b, 64 * b + 64), V("yt", b, 256, 4), 32.0)
+        half = ((0, 18), (18, 36))
+        for a, b in half:
+            act(V("ei", 16 * a, 16 * b), ind(V("w"), V("LI", a, b)))
+        for b in range(4):
+            act(V("fx", b, 1536, 4), V("fh", CW * b, CW * b + 384), 2.0)
+        for b in range(4):
+            ts(V("so", 4 * b, 4 * b + 4), V("kk", 181, 728, 182), 4.0, A.mult, 16384.0 + b, A.add)
+        for a, b in half:
+            tt(V("pr", 16 * a, 16 * b), ind(V("w"), V("LJ", a, b)), V("ei", 16 * a, 16 * b), A.mult)
+        scan(V("s5"), V("sg"), V("pr"), 0.0, A.mult, A.add)
+        tt(V("sp"), V("s5", 3, 576, 4), V("pw"), A.add)
+        ts(V("pw"), V("sp"), -3.0, A.max, 3.0, A.min)
+        if t < R - 1:
+            penalties()
+            weights()
+            late = direct
+            if not late:
+                table_p()
+                table_b()
+        else:
+            act(V("win1", 0, 144), V("pw"))
+            act(V("win1", 144, 288), V("pw"), -1.0)
+            act(V("tb1"), ind(V("win1"), L0))
+            for x in range(2):
+                for e in range(12):
+                    act(V("ob", 144 * x + e, 144 * x + 144, 12), V("tb1", 182 * x + e, 182 * x + 168, 14))
+            dma("y", T.oa[:], T.ob[:], V("ob")[1], [])
+            quant(V("vq"), V("vs"), V("vt0"))
+        sender = route(T, topo, (rank - 1) % N)
+        for sem, k in (("ac%d" % t, sender[2]), ("ap%d" % t, sender[3])):
+            count[sem] = len(topo.engines(sender[0] if k is None else k, core))
+            need("t", sem, count[sem], {})
+        for b in range(4):
+            mm(V("psE", 512 * b, 512 * b + 128), V("wq", 128 * b, 128 * b + 128), V("wp", 128 * b, 128 * b + 128), V("lc%d" % t), V("lp%d" % t))
+        for b in range(4):
+            tt(V("vf", 64 * b, 64 * b + 64), V("psE", 512 * b, 512 * b + 64), V("y32", 64 * b, 64 * b + 64), A.add)
+            if b % 2:
+                ts(V("vt", 64 * b - 64, 64 * b + 64), V("vf", 64 * b - 64, 64 * b + 64), 0.03125, A.mult)
+        run("v", lambda e: e.tensor_copy(T.fx[:, 0:1664].indirect(T.so[:, 0:16]), T.vt[:]), [V("vt"), V("so")], [V("fx")])
+
+    score_products(V("vq"), V("vs"))
+    dma("y", T.oc[:], u8(T, "xq", 0, 384), V("xq")[1], [])
+    for k in range(4):
+        dma("y", T.osc[4 * k:4 * k + 4, :], T.xs[32 * k:32 * k + 4, :], V("xs")[1], [])
+    for k in range(3):
+        cp(V("ysb", 128 * k, 128 * k + 128), V("psP", 512 * k, 512 * k + 128))
+    dma("s", T.y[:], T.ysb[:], V("ysb")[1], [])
+    for sem in count:
+        need("g", sem, count[sem], {})

@@ -5,6 +5,7 @@ BIG = 2.0 ** 90
 PEN, NONE = 2.0 ** 80, 2.0 ** 79
 Q = 8192.0
 CW = 416
+WAKE, NEAR, FAR = 120.0, 3000.0, 6200.0
 SCRATCH, CODES = {}, set()
 
 
@@ -17,18 +18,18 @@ def declare(dtype, spec):
             CODES.add(name)
 
 
-declare("bfloat16", "fx:1664 fh:1664 ut:512 vt0:512 yt:512 zt:512 et:520 ones:128 ga:512 gk:256 gs:512 gm2:256 y32:256 vt:256 "
+declare("bfloat16", "fx:1664 fh:1664 ut:512 vt0:512 yt:512 zt:512 et:520 ones:128 ga:512 sa:768 sb:768 sy:768 y32:256 vt:256 "
         "h1:364 h2:364 pw:144 w:104 pp:52 nn:52 oo:52 ei:576 pr:576 s5:576 sp:144 iC:384 cap:384 we:182 rs2:384 sg:576")
 declare("float8_e4m3fn_x4", "uq:128 urq:128 vq:128 eq:512 zq:128 wq:512 xq:384 " + " ".join("yc%d:128 lc%d:128 rc%d:64" % (t, t, t) for t in range(R)))
 declare("uint8", "us:128 urs:128 vs:128 es:512 zs:128 wp:512 xs:384 " + " ".join("yp%d:128 lp%d:128 rp%d:64" % (t, t, t) for t in range(R)))
 declare("float32", "psP:1536 psE:2048 vf:256 psc:384 gm:384 sc:384 pm1:24 ix:4 junk:64 s2:364 pm2:26 kk:728 ka:104 pmb:105 mn:104 sm:104 "
-        "bt:368 pen:368 win1:344 win2:344 tb1:368 tp0:368 ob:288 ysb:384 rt:384 nlf:24 iK:384 pf:4 pd:8 it13:13 k2i:24 k2c:52 cli:24 "
+        "bt:368 pen:368 win1:344 win2:344 tb1:368 tp0:368 ob:288 ysb:384 rt:384 iK:384 nlf:24 pf:4 pd:8 it13:13 k2i:24 k2c:52 "
         "rsx:160 lm:46 lA:46 lB:46 lC:46 lD:46 lE:46 lF:46 lG:46 lH:46 lI:46 uA:36 uX:36 uY:36 uZ:36 uB:36 uC:36")
 declare("int32", "di:16 dj:16 ndi:24 ari:288 pI:4 pA:4 ui:8 li:46")
-declare("uint16", "oL:20 so:16 nd16:24 nl:24 cl:24 ul:8 L:156")
+declare("uint16", "oL:20 so:16 nd16:24 nl:24 ul:8 L:156")
 PART = {"oA": ("oL", 0, 8), "oB": ("oL", 8, 8), "oK": ("oL", 16, 4), "rs24": ("rsx", 0, 24), "rs26": ("rsx", 24, 26), "rsk": ("rsx", 52, 104),
         "LI": ("L", 48, 36), "LJ": ("L", 84, 36), "L4": ("L", 120, 36)}
-DMAS = 24
+DMAS = 26
 SEMAPHORES = ["qv", "qs", "qt", "qg", "sent"] + ["d%d" % i for i in range(DMAS)] + ["ac%d" % t for t in range(R)] + ["ap%d" % t for t in range(R)]
 
 
@@ -81,8 +82,79 @@ def rank_program(g, core, T, topo):
     queue = {"v": g.vector, "s": g.scalar, "t": g.tensor, "g": g, "y": g.sync}
     count = {}
     known = {k: {} for k in queue}
-    log = {}
+    direct = route(T, topo, (rank - 1) % N)[2] is None
     free = ["d%d" % i for i in range(DMAS)]
+    ops, last = [], {}
+
+    def add(q, call, reads, writes, cost, sem=None, inc=1, after=(), arrivals=(), lag=0.0):
+        k = len(ops)
+        deps = {d: lag for d in after}
+        for kind, regions in (("r", reads), ("w", writes)):
+            for x in regions:
+                for o, y, d in last.get(x[0], []):
+                    if (kind == "w" or o == "w") and overlap(x, y):
+                        deps.setdefault(d, 0.0)
+        for x in writes:
+            last[x[0]] = [e for e in last.get(x[0], []) if not (e[1][1] >= x[1] and e[1][2] <= x[2] and x[3] == 1)]
+        for kind, regions in (("r", reads), ("w", writes)):
+            for x in regions:
+                last.setdefault(x[0], []).append((kind, x, k))
+        ops.append((q, call, cost, sem or "q" + q, inc, deps, arrivals))
+        return k
+
+    def run(q, call, reads, writes, cost, arr=None):
+        reads = [x for o in reads for x in o[1]]
+        writes = [x for o in writes for x in o[1]]
+        both = [x for x in reads if x[0] in ("psP", "psE")]
+        add(q, lambda e: call(e).then_inc(T.sem["q" + q], 1), [x for x in reads if x not in both], writes + both, cost,
+            after=[arr[0]] if arr else (), arrivals=arr[1] if arr else (), lag=(NEAR if direct else FAR) if arr else 0.0)
+
+    def dma(q, out, in_, reads, writes):
+        sem = free.pop(0)
+        add(q, lambda e: e.dma_start(out, in_).then_inc(T.sem[sem], 16), reads, writes, 2700.0, sem, 16)
+
+    def post(writes):
+        def call(e):
+            for to, out, mine, sem in writes:
+                count["sent"] = count.get("sent", 0) + send(e, T, topo, core, to, out, mine, sem)
+        return add("g", call, [(w[2], 0, 128, 1) for w in writes], [], 1400.0, "sent", 0)
+
+    def issue():
+        n = len(ops)
+        users = [[] for _ in range(n)]
+        far = [0.0] * n
+        for k in range(n):
+            for d in ops[k][5]:
+                users[d].append(k)
+        for k in range(n - 1, -1, -1):
+            far[k] = ops[k][2] + max([far[u] + WAKE + ops[u][5][k] for u in users[k]] or [0.0])
+        line = {q: [] for q in queue}
+        start = [0.0] * n
+        for k in sorted(range(n), key=lambda k: (-far[k], k)):
+            q, cost, deps = ops[k][0], ops[k][2], ops[k][5]
+            t0 = max([start[d] + ops[d][2] + WAKE + deps[d] for d in deps] or [0.0])
+            busy = 60.0 if ops[k][4] == 16 else cost
+            at = 0
+            for a, b in line[q]:
+                if t0 + busy <= a:
+                    break
+                t0 = max(t0, b)
+                at += 1
+            line[q].insert(at, (t0, t0 + busy))
+            start[k] = t0
+        mark = [None] * n
+        for k in sorted(range(n), key=lambda k: (start[k], -far[k], k)):
+            q, call, cost, sem, inc, deps, arrivals = ops[k]
+            for d in sorted(deps, key=lambda d: -mark[d][1]):
+                if mark[d][0] != "sent":
+                    need(q, *mark[d])
+            for a, v in arrivals:
+                need(q, a, v, {})
+                count[a] = v
+            call(queue[q])
+            if inc:
+                count[sem] = count.get(sem, 0) + inc
+            mark[k] = (sem, count.get(sem, 0), dict(known[q]))
 
     def need(q, sem, val, clock):
         if known[q].get(sem, 0) < val:
@@ -91,43 +163,6 @@ def rank_program(g, core, T, topo):
             for s in clock:
                 known[q][s] = max(known[q].get(s, 0), clock[s])
 
-    def waits(q, reads, writes):
-        w = []
-        for kind, regions in (("r", reads), ("w", writes)):
-            for x in regions:
-                for k, y, sem, val, clock in log.get(x[0], []):
-                    if (kind == "w" or k == "w") and overlap(x, y):
-                        w.append((sem, val, clock))
-        w.sort(key=lambda e: -e[1])
-        for sem, val, clock in w:
-            need(q, sem, val, clock)
-
-    def note(q, reads, writes, sem, val):
-        clock = dict(known[q])
-        for x in writes:
-            log[x[0]] = [e for e in log.get(x[0], []) if not (e[1][1] >= x[1] and e[1][2] <= x[2] and x[3] == 1)]
-        for kind, regions in (("r", reads), ("w", writes)):
-            for x in regions:
-                log.setdefault(x[0], []).append((kind, x, sem, val, clock))
-
-    def run(q, call, reads, writes):
-        reads = [x for o in reads for x in o[1]]
-        writes = [x for o in writes for x in o[1]]
-        both = [x for x in reads if x[0] in ("psP", "psE")]
-        reads = [x for x in reads if x not in both]
-        waits(q, reads + both, writes + both)
-        sem = "q" + q
-        count[sem] = count.get(sem, 0) + 1
-        call(queue[q]).then_inc(T.sem[sem], 1)
-        note(q, reads, writes + both, sem, count[sem])
-
-    def dma(q, out, in_, reads, writes):
-        waits(q, reads, writes)
-        sem = free.pop(0)
-        count[sem] = 16
-        queue[q].dma_start(out, in_).then_inc(T.sem[sem], 16)
-        note(q, reads, writes, sem, 16)
-
     def V(name, a=0, b=None, step=1):
         name, o, n = PART.get(name, (name, 0, None))
         b = (SCRATCH[name][1][1] if n is None else n) if b is None else b
@@ -135,7 +170,7 @@ def rank_program(g, core, T, topo):
         return (T[name][:, a:b:step] if step > 1 else T[name][:, a:b], [(name, a, b, step)])
 
     def ind(win, off):
-        return (win[0].indirect(off[0]), win[1] + off[1])
+        return (win[0].indirect(off[0]), win[1] + off[1], True)
 
     def val(s):
         return s[0] if isinstance(s, tuple) else s
@@ -143,29 +178,38 @@ def rank_program(g, core, T, topo):
     def reg(*ss):
         return [s for s in ss if isinstance(s, tuple)]
 
+    def size(v):
+        name, a, b, step = v[1][0]
+        return (b - a + step - 1) // step
+
+    def fast(n, *v):
+        return max(64, n * (0.5 if all(SCRATCH[x[1][0][0]][2] in ("bfloat16", "uint16") for x in v) else 1))
+
     def tt(out, a, b, op):
-        run("v", lambda e: e.tensor_tensor(out[0], a[0], b[0], op), [a, b], [out])
+        n = size(out)
+        cost = 50 + 1.6 * n if len(a) > 2 else max(64, n if a[1][0][0] in ("psP", "psE") else 2 * n)
+        run("v", lambda e: e.tensor_tensor(out[0], a[0], b[0], op), [a, b], [out], cost)
 
     def ts(out, a, s1, op0, s2=None, op1=None):
         if op1 is None:
-            run("v", lambda e: e.tensor_scalar(out[0], a[0], val(s1), None, op0), [a] + reg(s1), [out])
+            run("v", lambda e: e.tensor_scalar(out[0], a[0], val(s1), None, op0), [a] + reg(s1), [out], fast(size(out), a, out))
         else:
-            run("v", lambda e: e.tensor_scalar(out[0], a[0], val(s1), val(s2), op0, op1), [a] + reg(s1, s2), [out])
+            run("v", lambda e: e.tensor_scalar(out[0], a[0], val(s1), val(s2), op0, op1), [a] + reg(s1, s2), [out], fast(size(out), a, out))
 
     def cp(out, a):
-        run("v", lambda e: e.tensor_copy(out[0], a[0]), [a], [out])
+        run("v", lambda e: e.tensor_copy(out[0], a[0]), [a], [out], fast(size(out), a, out))
 
     def scan(out, d0, d1, initial, op0, op1):
-        run("v", lambda e: e.tensor_tensor_scan(out[0], d0[0], d1[0], initial, op0, op1), [d0, d1], [out])
+        run("v", lambda e: e.tensor_tensor_scan(out[0], d0[0], d1[0], initial, op0, op1), [d0, d1], [out], fast(size(out), d0, d1, out))
 
     def fill(out, c):
-        run("v", lambda e: e.memset(out[0], c), [], [out])
+        run("v", lambda e: e.memset(out[0], c), [], [out], max(64, size(out)))
 
     def quant(q, s, t):
-        run("v", lambda e: e.quantize_mx(q[0], s[0], t[0]), [t], [q, s])
+        run("v", lambda e: e.quantize_mx(q[0], s[0], t[0]), [t], [q, s], 15 + 0.26 * size(t))
 
-    def mm(out, w, ws, x, xs):
-        run("t", lambda e: e.matmul_mx(out[0], w[0], ws[0], x[0], xs[0], True, True), [w, ws, x, xs], [out])
+    def mm(out, w, ws, x, xs, arr=None):
+        run("t", lambda e: e.matmul_mx(out[0], w[0], ws[0], x[0], xs[0], True, True), [w, ws, x, xs], [out], 1.7 * size(x) + 18, arr)
 
     def act(out, a, scale=1.0, func=None, bias=None, accum=None):
         kw = {}
@@ -176,16 +220,18 @@ def rank_program(g, core, T, topo):
             func = func or F.Identity
         if accum is not None:
             kw["accum_out"] = accum[0]
-        run("s", lambda e: e.activation(out[0], a[0], func or F.Copy, **kw), [a] + reg(bias), [out] + reg(accum))
+        run("s", lambda e: e.activation(out[0], a[0], func or F.Copy, **kw), [a] + reg(bias), [out] + reg(accum),
+            70 + 1.6 * size(out) if len(a) > 2 else max(64, size(out)) + (20 if accum is not None else 0))
 
     def iota(out, pattern, base=0, cm=0):
+        cost = 150 + 2 * size(out)
         if SCRATCH[out[1][0][0]][2] == "int32":
-            run("g", lambda e: e.iota(out[0], pattern, base, cm), [], [out])
+            run("g", lambda e: e.iota(out[0], pattern, base, cm), [], [out], cost)
         else:
-            run("g", lambda e: e.iota(out[0], pattern, base, cm, allow_small_or_imprecise_dtypes=True), [], [out])
+            run("g", lambda e: e.iota(out[0], pattern, base, cm, allow_small_or_imprecise_dtypes=True), [], [out], cost)
 
     def select(out, pattern, fill_, base):
-        run("g", lambda e: e.affine_select(out[0], out[0], pattern, A.not_equal, fill_, base, 0), [out], [out])
+        run("g", lambda e: e.affine_select(out[0], out[0], pattern, A.not_equal, fill_, base, 0), [out], [out], 200 + 2 * size(out))
 
     dma("y", T.ndi[:], T.nd[:], [], V("ndi")[1])
     dma("s", T.ut[:], T.u[:], [], V("ut")[1])
@@ -197,21 +243,20 @@ def rank_program(g, core, T, topo):
     dma("y", T.vt0[:], T.v[:], [], V("vt0")[1])
 
     lm = lambda n, a=0, b=46: V(n, a, b)
-    fill(V("ones"), 1.0)
-    fill(V("et"), 0.0)
-    fill(V("rsx"), BIG)
     iota(V("pI"), [[0, 4]], 0, 1)
     iota(lm("lm"), [[0, 2], [16, 23]])
-    iota(V("cli"), [[192, 2], [1, 12]])
     iota(V("uA"), [[0, 2], [1, 6], [4, 3]], 1)
     iota(V("uZ"), [[144, 2], [0, 6], [48, 3]])
     iota(V("iK"), [[1, 384]])
     iota(V("iC"), [[0, 24], [1, 16]])
     iota(V("ui"), [[16, 8]])
-    run("g", lambda e: e.affine_select(T.et[:, 3:515:4], T.ones[:], [[-1, 128]], A.is_equal, 0.0, 0, 1), [V("ones")], [V("et")])
+    iota(V("ones"), [[0, 128]], 1)
+    iota(V("et"), [[0, 520]])
+    run("g", lambda e: e.affine_select(T.et[:, 3:515:4], T.ones[:], [[-1, 128]], A.is_equal, 0.0, 0, 1), [V("ones")], [V("et")], 460.0)
     iota(V("k2i"), [[0, 2], [-512, 12]], -512)
     for n in ("win1", "win2"):
         iota(V(n, 288, 344), [[0, 56]])
+    act(V("rsx"), V("iC", 0, 160), 0.0, bias=BIG)
     for k, c in ((1, PEN), (39, NONE), (53, NONE)):
         select(V("win2", 288, 344), [[1, 56]], c, -k)
     select(V("rs24"), [[0, 2], [1, 12]], -BIG, 0)
@@ -225,6 +270,9 @@ def rank_program(g, core, T, topo):
     iota(V("uX"), [[13, 2], [0, 18]])
     iota(V("uY"), [[13, 2], [0, 6], [4, 3]])
     iota(V("it13"), [[1, 13]])
+    iota(V("sb", 0, 768, 3), [[0, 256]])
+    act(V("sa", 2, 768, 3), V("iC", 0, 256), 0.0, bias=-BIG)
+    act(V("sb", 2, 768, 3), V("iC", 0, 256), 0.0, bias=BIG)
     iota(V("zt"), [[0, 512]])
 
     ts(V("pA", 0, 1), V("pI", 0, 1), 15, A.bitwise_and)
@@ -234,17 +282,15 @@ def rank_program(g, core, T, topo):
     cp(V("pf"), V("pA"))
     p16, p4, pt, p1 = (V("pf", k, k + 1) for k in range(4))
     act(V("pd", 2, 3), p16, -1.0, bias=182.0)
-    act(V("pd", 0, 1), p16, 12.0)
     act(V("pd", 5, 6), p4, 12.0)
     act(V("uB"), V("uA"), bias=p4)
     ts(lm("lB"), lm("lm"), V("pd", 2, 3), A.is_ge)
-    ts(V("cl"), V("cli"), V("pd", 0, 1), A.add)
     ts(lm("lC"), lm("lB"), -182.0, A.mult, p16, A.add)
     ts(V("uC"), V("uB"), 12.0, A.is_ge, -12.0, A.mult)
     tt(lm("lD"), lm("lC"), lm("lm"), A.add)
     tt(V("uC"), V("uC"), V("uB"), A.add)
     ts(lm("li"), lm("lD"), 1.0 / 14, A.mult, -6.5 / 14, A.add)
-    fill(V("pmb", 0, 1), -BIG)
+    act(V("pmb", 0, 1), p16, 0.0, bias=-BIG)
     cp(lm("lE"), lm("li"))
     tt(V("uZ"), V("uZ"), V("uC"), A.add)
     ts(lm("lC"), lm("lE"), -14.0, A.mult)
@@ -268,21 +314,21 @@ def rank_program(g, core, T, topo):
 
     cp(V("nd16"), V("ndi"))
     act(V("rt"), ind(V("iK"), V("nd16")))
+    for x in range(2):
+        dma("y", T.nlf[:, 12 * x:12 * x + 12], T.rt[0:128:16, 192 * x:192 * x + 192], V("rt")[1], V("nlf", 12 * x, 12 * x + 12)[1])
     act(V("cap"), V("iC"), -1.0, F.Square, p16)
     act(V("cap"), V("cap"), -2.0 * BIG, bias=BIG)
-    fill(V("rs2"), BIG)
+    act(V("rs2"), V("iC"), 0.0, bias=BIG)
     cp(V("ul"), V("ui"))
     fill(V("rs2", 0, 384, 16), -BIG)
     quant(V("uq"), V("us"), V("ut"))
-    run("v", lambda e: e.tensor_copy(T.urq[:, 0:128].bitcast(dt.uint32), T.uq[:, 0:128].bitcast(dt.uint32).indirect(T.ul[:, 0:8])), [V("uq"), V("ul")], [V("urq")])
+    run("v", lambda e: e.tensor_copy(T.urq[:, 0:128].bitcast(dt.uint32), T.uq[:, 0:128].bitcast(dt.uint32).indirect(T.ul[:, 0:8])),
+        [V("uq"), V("ul")], [V("urq")], 250.0)
     act(V("urs"), ind(V("us"), V("ul")))
     score_products(V("urq"), V("urs"))
-    tt(V("gm"), ind(V("rt"), V("cl")), V("cap"), A.min)
     act(V("ei"), ind(V("ari"), V("L4")))
-    scan(V("sc"), V("rs2"), V("gm"), -BIG, A.min, A.max)
     act(V("pw"), V("ei", 0, 576, 4))
-    cp(V("nl"), V("sc", 15, 384, 16))
-    act(V("nlf"), V("sc", 15, 384, 16))
+    cp(V("nl"), V("nlf"))
     act(lm("lG"), lm("lC"), 12.0, bias=-12.0)
     act(lm("lD"), lm("lC"), -12.0, bias=276.0)
     ts(lm("lH"), lm("lC"), 7.0, A.is_ge, 1000.0, A.mult)
@@ -328,8 +374,6 @@ def rank_program(g, core, T, topo):
     def table_b():
         tt(V("bt"), ind(V("win1"), L0), V("tb1"), A.subtract)
 
-    direct = route(T, topo, (rank - 1) % N)[2] is None
-    late = True
     for t in range(R):
         if t:
             score_products(V("urq"), V("urs"))
@@ -345,52 +389,42 @@ def rank_program(g, core, T, topo):
                 end = n * x + n - 1
                 act(V("junk", 16 * (k + x), 16 * (k + x) + n), V(src, n * x, end + 1), -1.0, F.Sign, V(src, end, end + 1), V("ix", k + x, k + x + 1))
 
-        if t:
-            unpack(0)
-            unpack(1)
         tt(V("gm"), ind(V("psc"), V("nl")), V("cap"), A.min)
         if t == 0:
             tt(V("win1", 290, 314), V("nlf"), V("k2i"), A.add)
-            penalties()
-        scan(V("sc"), V("rs2"), V("gm"), -BIG, A.min, A.max)
-        scan(V("pm1"), V("rs24"), V("sc", 15, 384, 16), -BIG, A.min, A.max)
-        which("pm1", 12, 0)
-        if late:
-            table_p()
-        for x in range(2):
-            cp(V("pen", 182 * x + 13, 182 * x + 13 + 155, 14), V("sc", 192 * x + 15, 192 * x + 192, 16))
-        if t:
-            unpack(2)
-            unpack(3)
-        else:
             for x in range(2):
                 act(V("win1", 314 + 14 * x, 326 + 14 * x), V("nlf", 12 * x, 12 * x + 12), bias=-4096.0)
                 act(V("win1", 326 + 14 * x, 327 + 14 * x), p16, bias=384.0 + 16 * x - 4096.0)
+            penalties()
             weights()
+            table_p()
+            table_b()
             for x in range(4):
                 act(V("k2c", 13 * x, 13 * x + 12), V("win1", 290 + 12 * (x % 2), 302 + 12 * (x % 2)))
             for b in range(4):
                 quant(V("eq", 128 * b, 128 * b + 128), V("es", 128 * b, 128 * b + 128), V("et", 3 - b, 515 - b))
             unpack_products()
+        for b in range(4):
+            unpack(b)
+        scan(V("sc"), V("rs2"), V("gm"), -BIG, A.min, A.max)
+        scan(V("pm1"), V("rs24"), V("sc", 15, 384, 16), -BIG, A.min, A.max)
+        which("pm1", 12, 0)
+        for x in range(2):
+            cp(V("pen", 182 * x + 13, 182 * x + 13 + 155, 14), V("sc", 192 * x + 15, 192 * x + 192, 16))
         for x in range(2):
             ts(V("h1", 182 * x, 182 * x + 182), V("we"), V("ix", x, x + 1), A.is_gt)
         scan(V("s2"), V("h1"), V("pen", 0, 364), 0.0, A.mult, A.add)
         scan(V("pm2"), V("rs26"), V("s2", 13, 364, 14), -BIG, A.min, A.max)
         which("pm2", 13, 2)
-        if late:
-            table_b()
-        if t == 0:
-            for b in range(4):
-                unpack(b)
         scan(V("kk", 0, 364), V("h1"), V("bt", 0, 364), 0.0, A.mult, A.add)
         for x in range(2):
             ts(V("h2", 182 * x, 182 * x + 182), V("we"), V("ix", 2 + x, 3 + x), A.is_gt)
         scan(V("kk", 364, 728), V("h2"), V("bt", 0, 364), 0.0, A.mult, A.add)
         tt(V("ka", 52, 104), V("k2c"), V("kk", 12, 728, 14), A.subtract)
-        cp(V("ka", 0, 52), V("kk", 13, 728, 14))
+        act(V("ka", 0, 52), V("kk", 13, 728, 14))
         ts(V("oK"), V("kk", 181, 728, 182), 4096.0, A.add)
         for b in range(4):
-            act(V("gk", 64 * b, 64 * b + 64), ind(V("fh", CW * b, CW * b + CW), V("oK")), 2.0)
+            act(V("sb", 3 * b + 1, 768, 12), ind(V("fh", CW * b, CW * b + CW), V("oK")), 2.0)
         scan(V("pmb", 1, 105), V("rsk"), V("ka"), -BIG, A.min, A.max)
         ts(V("di", 0, 8), V("pmb", 12, 105, 13), 384.0, A.max)
         tt(V("mn"), V("ka"), V("pmb", 0, 104), A.min)
@@ -403,18 +437,14 @@ def rank_program(g, core, T, topo):
         ts(V("dj", 8, 16), V("di", 8, 16), 511, A.bitwise_and)
         cp(V("oB"), V("dj", 8, 16))
         for b in range(4):
-            tt(V("gs", 128 * b, 128 * b + 128), ind(V("fh", CW * b, CW * b + CW), V("oB")), V("ga", 128 * b, 128 * b + 128), A.add)
-            if b:
-                tt(V("gm2", 64 * b - 64, 64 * b), V("gs", 128 * b - 128, 128 * b - 64), V("gs", 128 * b - 64, 128 * b), A.max)
-        tt(V("yt", 0, 256, 4), V("gm2", 0, 64), V("gk", 0, 64), A.subtract)
-        tt(V("gm2", 192, 256), V("gs", 384, 448), V("gs", 448, 512), A.max)
-        for b in range(1, 4):
-            tt(V("yt", b, 256, 4), V("gm2", 64 * b, 64 * b + 64), V("gk", 64 * b, 64 * b + 64), A.subtract)
+            for k in range(2):
+                tt(V("sa", 3 * b + k, 768, 12), ind(V("fh", CW * b, CW * b + CW), V("oB", 4 * k, 4 * k + 4)), V("ga", 128 * b + 64 * k, 128 * b + 64 * k + 64), A.add)
+        scan(V("sy"), V("sa"), V("sb"), -BIG, A.max, A.subtract)
+        cp(V("yt", 0, 256), V("sy", 1, 768, 3))
         quant(V("yc%d" % t), V("yp%d" % t), V("yt"))
-        waits("g", [("yc%d" % t, 0, 128, 1), ("yp%d" % t, 0, 128, 1)], [])
         src, dst, ca, cb = route(T, topo, rank)
-        for k, sem, mid, out, mine in ((ca, "ac%d" % t, "rc%d" % t, "lc%d" % t, "yc%d" % t), (cb, "ap%d" % t, "rp%d" % t, "lp%d" % t, "yp%d" % t)):
-            count["sent"] = count.get("sent", 0) + send(g, T, topo, core, dst if k is None else k, out if k is None else mid, mine, sem)
+        sent = post([(dst if k is None else k, (out if k is None else mid) + str(t), mine + str(t), sem + str(t))
+                     for k, sem, mid, out, mine in ((ca, "ac", "rc", "lc", "yc"), (cb, "ap", "rp", "lp", "yp"))])
         for f in range(2):
             for x in range(2):
                 ts(V("oo", 26 * f + 13 * x, 26 * f + 13 * x + 13), V("it13"), V("ix", 2 * f + x, 2 * f + x + 1), A.is_equal, -2.0, A.mult)
@@ -455,10 +485,8 @@ def rank_program(g, core, T, topo):
         if t < R - 1:
             penalties()
             weights()
-            late = direct
-            if not late:
-                table_p()
-                table_b()
+            table_p()
+            table_b()
         else:
             act(V("win1", 0, 144), V("pw"))
             act(V("win1", 144, 288), V("pw"), -1.0)
@@ -468,17 +496,15 @@ def rank_program(g, core, T, topo):
                     act(V("ob", 144 * x + e, 144 * x + 144, 12), V("tb1", 182 * x + e, 182 * x + 168, 14))
             dma("y", T.oa[:], T.ob[:], V("ob")[1], [])
             quant(V("vq"), V("vs"), V("vt0"))
-        sender = route(T, topo, (rank - 1) % N)
+        sender, arr = route(T, topo, (rank - 1) % N), []
         for sem, k in (("ac%d" % t, sender[2]), ("ap%d" % t, sender[3])):
-            count[sem] = len(topo.engines(sender[0] if k is None else k, core))
-            need("t", sem, count[sem], {})
+            arr.append((sem, len(topo.engines(sender[0] if k is None else k, core))))
         for b in range(4):
-            mm(V("psE", 512 * b, 512 * b + 128), V("wq", 128 * b, 128 * b + 128), V("wp", 128 * b, 128 * b + 128), V("lc%d" % t), V("lp%d" % t))
+            mm(V("psE", 512 * b, 512 * b + 128), V("wq", 128 * b, 128 * b + 128), V("wp", 128 * b, 128 * b + 128), V("lc%d" % t), V("lp%d" % t), (sent, arr))
         for b in range(4):
             tt(V("vf", 64 * b, 64 * b + 64), V("psE", 512 * b, 512 * b + 64), V("y32", 64 * b, 64 * b + 64), A.add)
-            if b % 2:
-                ts(V("vt", 64 * b - 64, 64 * b + 64), V("vf", 64 * b - 64, 64 * b + 64), 0.03125, A.mult)
-        run("v", lambda e: e.tensor_copy(T.fx[:, 0:1664].indirect(T.so[:, 0:16]), T.vt[:]), [V("vt"), V("so")], [V("fx")])
+            ts(V("vt", 64 * b, 64 * b + 64), V("vf", 64 * b, 64 * b + 64), 0.03125, A.mult)
+        run("v", lambda e: e.tensor_copy(T.fx[:, 0:1664].indirect(T.so[:, 0:16]), T.vt[:]), [V("vt"), V("so")], [V("fx")], 1000.0)
 
     score_products(V("vq"), V("vs"))
     dma("y", T.oc[:], u8(T, "xq", 0, 384), V("xq")[1], [])
@@ -487,5 +513,6 @@ def rank_program(g, core, T, topo):
     for k in range(3):
         cp(V("ysb", 128 * k, 128 * k + 128), V("psP", 512 * k, 512 * k + 128))
     dma("s", T.y[:], T.ysb[:], V("ysb")[1], [])
+    issue()
     for sem in count:
         need("g", sem, count[sem], {})

from concourse.mybir import dt, AluOpType, ActivationFunctionType

N, C, R = 8, 384, 3
BIG = 2.0 ** 90
PEN, NONE = 2.0 ** 80, 2.0 ** 79
Q = 8192.0
CW = 416
WAKE, NEAR, FAR = 120.0, 3000.0, 6200.0
SCRATCH, CODES = {}, set()


def declare(dtype, spec):
    for item in spec.split():
        name, cols = item.split(":")
        where = "psum" if name in ("psP", "psE") else "sbuf"
        SCRATCH[name] = (where, [128, int(cols)], dtype)
        if dtype == "float8_e4m3fn_x4":
            CODES.add(name)


declare("bfloat16", "fx:1664 fh:1664 ut:512 vt0:512 yt:512 zt:512 et:520 ones:128 ga:512 sa:768 sb:768 sy:768 y32:256 vt:256 "
        "h1:364 h2:364 pw:144 w:104 pp:52 nn:52 oo:52 ei:576 pr:576 s5:576 sp:144 iC:384 cap:384 we:182 rs2:384 sg:576")
declare("float8_e4m3fn_x4", "uq:128 urq:128 vq:128 eq:512 zq:128 wq:512 xq:384 " + " ".join("yc%d:128 lc%d:128 rc%d:64" % (t, t, t) for t in range(R)))
declare("uint8", "us:128 urs:128 vs:128 es:512 zs:128 wp:512 xs:384 " + " ".join("yp%d:128 lp%d:128 rp%d:64" % (t, t, t) for t in range(R)))
declare("float32", "psP:1536 psE:2048 vf:256 psc:384 gm:384 sc:384 pm1:24 ix:4 junk:64 s2:364 pm2:26 kk:728 ka:104 pmb:105 mn:104 sm:104 "
        "bt:368 pen:368 win1:344 win2:344 tb1:368 tp0:368 ob:288 ysb:384 rt:384 iK:384 nlf:24 pf:4 pd:8 it13:13 k2i:24 k2c:52 "
        "rsx:160 lm:46 lA:46 lB:46 lC:46 lD:46 lE:46 lF:46 lG:46 lH:46 lI:46 uA:36 uX:36 uY:36 uZ:36 uB:36 uC:36")
declare("int32", "di:16 dj:16 ndi:24 ari:288 pI:4 pA:4 ui:8 li:46")
declare("uint16", "oL:20 so:16 nd16:24 nl:24 ul:8 L:156")
PART = {"oA": ("oL", 0, 8), "oB": ("oL", 8, 8), "oK": ("oL", 16, 4), "rs24": ("rsx", 0, 24), "rs26": ("rsx", 24, 26), "rsk": ("rsx", 52, 104),
        "LI": ("L", 48, 36), "LJ": ("L", 84, 36), "L4": ("L", 120, 36)}
DMAS = 26
SEMAPHORES = ["qv", "qs", "qt", "qg", "sent"] + ["d%d" % i for i in range(DMAS)] + ["ac%d" % t for t in range(R)] + ["ap%d" % t for t in range(R)]


def route(T, topo, r):
    src, dst = T.cores[r], T.cores[(r + 1) % N]
    if topo.may_write(src, dst):
        return src, dst, None, None
    c = [k for k in topo.cores_of(src) if k not in T.cores and topo.may_write(k, dst)]
    c.sort(key=lambda k: (topo.die(k) != topo.die(src), k))
    return src, dst, c[0], c[1 % len(c)]


def u8(T, name, a, b):
    v = T[name][:, a:b]
    return v.bitcast(dt.uint8) if name in CODES else v


def send(g, T, topo, core, to, out, src, sem):
    rid, pid = topo.addr(to, core)
    g.remote_dma(u8(T, out, 0, 64), u8(T, src, 0, 64), T.sem[sem], T.sem.sent, pid, rid, topo.mask(core, to))
    return len(topo.engines(core, to))


def relay_program(g, core, T, topo):
    total = 0
    for t in range(R):
        for r in range(N):
            src, dst, ca, cb = route(T, topo, r)
            for k, sem, mid, out in ((ca, "ac%d" % t, "rc%d" % t, "lc%d" % t), (cb, "ap%d" % t, "rp%d" % t, "lp%d" % t)):
                if k == core:
                    g.wait_ge(T.sem[sem], len(topo.engines(src, core)))
                    total += send(g, T, topo, core, dst, out, mid, sem)
    if total:
        g.wait_ge(T.sem.sent, total)


def overlap(a, b):
    if a[0] != b[0] or a[1] >= b[2] or b[1] >= a[2]:
        return False
    return not (a[3] == b[3] > 1 and (a[1] - b[1]) % a[3])


def rank_program(g, core, T, topo):
    rank = T.rank_of(core)
    if rank is None:
        relay_program(g, core, T, topo)
        return
    A = AluOpType
    F = ActivationFunctionType
    queue = {"v": g.vector, "s": g.scalar, "t": g.tensor, "g": g, "y": g.sync}
    count = {}
    known = {k: {} for k in queue}
    direct = route(T, topo, (rank - 1) % N)[2] is None
    free = ["d%d" % i for i in range(DMAS)]
    ops, last = [], {}

    def add(q, call, reads, writes, cost, sem=None, inc=1, after=(), arrivals=(), lag=0.0):
        k = len(ops)
        deps = {d: lag for d in after}
        for kind, regions in (("r", reads), ("w", writes)):
            for x in regions:
                for o, y, d in last.get(x[0], []):
                    if (kind == "w" or o == "w") and overlap(x, y):
                        deps.setdefault(d, 0.0)
        for x in writes:
            last[x[0]] = [e for e in last.get(x[0], []) if not (e[1][1] >= x[1] and e[1][2] <= x[2] and x[3] == 1)]
        for kind, regions in (("r", reads), ("w", writes)):
            for x in regions:
                last.setdefault(x[0], []).append((kind, x, k))
        ops.append((q, call, cost, sem or "q" + q, inc, deps, arrivals))
        return k

    def run(q, call, reads, writes, cost, arr=None):
        reads = [x for o in reads for x in o[1]]
        writes = [x for o in writes for x in o[1]]
        both = [x for x in reads if x[0] in ("psP", "psE")]
        add(q, lambda e: call(e).then_inc(T.sem["q" + q], 1), [x for x in reads if x not in both], writes + both, cost,
            after=[arr[0]] if arr else (), arrivals=arr[1] if arr else (), lag=(NEAR if direct else FAR) if arr else 0.0)

    def dma(q, out, in_, reads, writes):
        sem = free.pop(0)
        add(q, lambda e: e.dma_start(out, in_).then_inc(T.sem[sem], 16), reads, writes, 2700.0, sem, 16)

    def post(writes):
        def call(e):
            for to, out, mine, sem in writes:
                count["sent"] = count.get("sent", 0) + send(e, T, topo, core, to, out, mine, sem)
        return add("g", call, [(w[2], 0, 128, 1) for w in writes], [], 1400.0, "sent", 0)

    def issue():
        n = len(ops)
        users = [[] for _ in range(n)]
        far = [0.0] * n
        for k in range(n):
            for d in ops[k][5]:
                users[d].append(k)
        for k in range(n - 1, -1, -1):
            far[k] = ops[k][2] + max([far[u] + WAKE + ops[u][5][k] for u in users[k]] or [0.0])
        line = {q: [] for q in queue}
        start = [0.0] * n
        for k in sorted(range(n), key=lambda k: (-far[k], k)):
            q, cost, deps = ops[k][0], ops[k][2], ops[k][5]
            t0 = max([start[d] + ops[d][2] + WAKE + deps[d] for d in deps] or [0.0])
            busy = 60.0 if ops[k][4] == 16 else cost
            at = 0
            for a, b in line[q]:
                if t0 + busy <= a:
                    break
                t0 = max(t0, b)
                at += 1
            line[q].insert(at, (t0, t0 + busy))
            start[k] = t0
        mark = [None] * n
        for k in sorted(range(n), key=lambda k: (start[k], -far[k], k)):
            q, call, cost, sem, inc, deps, arrivals = ops[k]
            for d in sorted(deps, key=lambda d: -mark[d][1]):
                if mark[d][0] != "sent":
                    need(q, *mark[d])
            for a, v in arrivals:
                need(q, a, v, {})
                count[a] = v
            call(queue[q])
            if inc:
                count[sem] = count.get(sem, 0) + inc
            mark[k] = (sem, count.get(sem, 0), dict(known[q]))

    def need(q, sem, val, clock):
        if known[q].get(sem, 0) < val:
            queue[q].wait_ge(T.sem[sem], val)
            known[q][sem] = val
            for s in clock:
                known[q][s] = max(known[q].get(s, 0), clock[s])

    def V(name, a=0, b=None, step=1):
        name, o, n = PART.get(name, (name, 0, None))
        b = (SCRATCH[name][1][1] if n is None else n) if b is None else b
        a, b = a + o, b + o
        return (T[name][:, a:b:step] if step > 1 else T[name][:, a:b], [(name, a, b, step)])

    def ind(win, off):
        return (win[0].indirect(off[0]), win[1] + off[1], True)

    def val(s):
        return s[0] if isinstance(s, tuple) else s

    def reg(*ss):
        return [s for s in ss if isinstance(s, tuple)]

    def size(v):
        name, a, b, step = v[1][0]
        return (b - a + step - 1) // step

    def fast(n, *v):
        return max(64, n * (0.5 if all(SCRATCH[x[1][0][0]][2] in ("bfloat16", "uint16") for x in v) else 1))

    def tt(out, a, b, op):
        n = size(out)
        cost = 50 + 1.6 * n if len(a) > 2 else max(64, n if a[1][0][0] in ("psP", "psE") else 2 * n)
        run("v", lambda e: e.tensor_tensor(out[0], a[0], b[0], op), [a, b], [out], cost)

    def ts(out, a, s1, op0, s2=None, op1=None):
        if op1 is None:
            run("v", lambda e: e.tensor_scalar(out[0], a[0], val(s1), None, op0), [a] + reg(s1), [out], fast(size(out), a, out))
        else:
            run("v", lambda e: e.tensor_scalar(out[0], a[0], val(s1), val(s2), op0, op1), [a] + reg(s1, s2), [out], fast(size(out), a, out))

    def cp(out, a):
        run("v", lambda e: e.tensor_copy(out[0], a[0]), [a], [out], fast(size(out), a, out))

    def scan(out, d0, d1, initial, op0, op1):
        run("v", lambda e: e.tensor_tensor_scan(out[0], d0[0], d1[0], initial, op0, op1), [d0, d1], [out], fast(size(out), d0, d1, out))

    def fill(out, c):
        run("v", lambda e: e.memset(out[0], c), [], [out], max(64, size(out)))

    def quant(q, s, t):
        run("v", lambda e: e.quantize_mx(q[0], s[0], t[0]), [t], [q, s], 15 + 0.26 * size(t))

    def mm(out, w, ws, x, xs, arr=None):
        run("t", lambda e: e.matmul_mx(out[0], w[0], ws[0], x[0], xs[0], True, True), [w, ws, x, xs], [out], 1.7 * size(x) + 18, arr)

    def act(out, a, scale=1.0, func=None, bias=None, accum=None):
        kw = {}
        if scale != 1.0:
            kw["scale"] = scale
        if bias is not None:
            kw["bias"] = val(bias)
            func = func or F.Identity
        if accum is not None:
            kw["accum_out"] = accum[0]
        run("s", lambda e: e.activation(out[0], a[0], func or F.Copy, **kw), [a] + reg(bias), [out] + reg(accum),
            70 + 1.6 * size(out) if len(a) > 2 else max(64, size(out)) + (20 if accum is not None else 0))

    def iota(out, pattern, base=0, cm=0):
        cost = 150 + 2 * size(out)
        if SCRATCH[out[1][0][0]][2] == "int32":
            run("g", lambda e: e.iota(out[0], pattern, base, cm), [], [out], cost)
        else:
            run("g", lambda e: e.iota(out[0], pattern, base, cm, allow_small_or_imprecise_dtypes=True), [], [out], cost)

    def select(out, pattern, fill_, base):
        run("g", lambda e: e.affine_select(out[0], out[0], pattern, A.not_equal, fill_, base, 0), [out], [out], 200 + 2 * size(out))

    dma("y", T.ndi[:], T.nd[:], [], V("ndi")[1])
    dma("s", T.ut[:], T.u[:], [], V("ut")[1])
    dma("y", T.fx[:, 0:768], T.x[:, 0:768], [], V("fx", 0, 768)[1])
    dma("s", T.fx[:, 768:1536], T.x[:, 768:1536], [], V("fx", 768, 1536)[1])
    dma("y", T.ari[:], T.ar[:], [], V("ari")[1])
    dma("y", T.wq[:, 0:512].bitcast(dt.uint8), T.wc[:], [], V("wq")[1])
    dma("y", T.wp[:], T.ws[:], [], V("wp")[1])
    dma("y", T.vt0[:], T.v[:], [], V("vt0")[1])

    lm = lambda n, a=0, b=46: V(n, a, b)
    iota(V("pI"), [[0, 4]], 0, 1)
    iota(lm("lm"), [[0, 2], [16, 23]])
    iota(V("uA"), [[0, 2], [1, 6], [4, 3]], 1)
    iota(V("uZ"), [[144, 2], [0, 6], [48, 3]])
    iota(V("iK"), [[1, 384]])
    iota(V("iC"), [[0, 24], [1, 16]])
    iota(V("ui"), [[16, 8]])
    iota(V("ones"), [[0, 128]], 1)
    iota(V("et"), [[0, 520]])
    run("g", lambda e: e.affine_select(T.et[:, 3:515:4], T.ones[:], [[-1, 128]], A.is_equal, 0.0, 0, 1), [V("ones")], [V("et")], 460.0)
    iota(V("k2i"), [[0, 2], [-512, 12]], -512)
    for n in ("win1", "win2"):
        iota(V(n, 288, 344), [[0, 56]])
    act(V("rsx"), V("iC", 0, 160), 0.0, bias=BIG)
    for k, c in ((1, PEN), (39, NONE), (53, NONE)):
        select(V("win2", 288, 344), [[1, 56]], c, -k)
    select(V("rs24"), [[0, 2], [1, 12]], -BIG, 0)
    select(V("rs26"), [[0, 2], [1, 13]], -BIG, 0)
    iota(V("we"), [[0, 13], [1, 14]])
    iota(V("k2c"), [[0, 52]], -8192)
    select(V("rsk"), [[0, 8], [1, 13]], -BIG, -12)
    for b in range(4):
        iota(V("fh", CW * b + 384, CW * b + CW), [[0, 32]])
    iota(V("yt", 256, 512), [[0, 256]])
    iota(V("uX"), [[13, 2], [0, 18]])
    iota(V("uY"), [[13, 2], [0, 6], [4, 3]])
    iota(V("it13"), [[1, 13]])
    iota(V("sb", 0, 768, 3), [[0, 256]])
    act(V("sa", 2, 768, 3), V("iC", 0, 256), 0.0, bias=-BIG)
    act(V("sb", 2, 768, 3), V("iC", 0, 256), 0.0, bias=BIG)
    iota(V("zt"), [[0, 512]])

    ts(V("pA", 0, 1), V("pI", 0, 1), 15, A.bitwise_and)
    ts(V("pA", 1, 2), V("pI", 1, 2), 2, A.logical_shift_right, 3, A.bitwise_and)
    ts(V("pA", 2, 3), V("pI", 2, 3), 3, A.bitwise_and)
    ts(V("pA", 3, 4), V("pI", 3, 4), 1, A.bitwise_and)
    cp(V("pf"), V("pA"))
    p16, p4, pt, p1 = (V("pf", k, k + 1) for k in range(4))
    act(V("pd", 2, 3), p16, -1.0, bias=182.0)
    act(V("pd", 5, 6), p4, 12.0)
    act(V("uB"), V("uA"), bias=p4)
    ts(lm("lB"), lm("lm"), V("pd", 2, 3), A.is_ge)
    ts(lm("lC"), lm("lB"), -182.0, A.mult, p16, A.add)
    ts(V("uC"), V("uB"), 12.0, A.is_ge, -12.0, A.mult)
    tt(lm("lD"), lm("lC"), lm("lm"), A.add)
    tt(V("uC"), V("uC"), V("uB"), A.add)
    ts(lm("li"), lm("lD"), 1.0 / 14, A.mult, -6.5 / 14, A.add)
    act(V("pmb", 0, 1), p16, 0.0, bias=-BIG)
    cp(lm("lE"), lm("li"))
    tt(V("uZ"), V("uZ"), V("uC"), A.add)
    ts(lm("lC"), lm("lE"), -14.0, A.mult)
    ts(V("L4"), V("uZ"), V("pd", 5, 6), A.add)
    tt(lm("lF"), lm("lC"), lm("lD"), A.add)
    ts(lm("lF", 23, 46), lm("lF", 23, 46), 1.0, A.add)
    tt(lm("lC"), lm("lF"), lm("lE"), A.subtract)
    act(lm("lI"), lm("lB"), 72.0)
    ts(lm("lD"), lm("lC"), 0.0, A.is_lt, 12.0, A.mult)
    tt(lm("lC"), lm("lC"), lm("lD"), A.add)

    def score_products(w, ws):
        for k in range(3):
            a = 128 * k
            quant(V("xq", a, a + 128), V("xs", a, a + 128), V("fx", 4 * a, 4 * a + 512))
            mm(V("psP", 512 * k, 512 * k + 128), w, ws, V("xq", a, a + 128), V("xs", a, a + 128))

    def unpack_products():
        for b in range(4):
            mm(V("psE", 512 * b, 512 * b + 384), V("eq", 128 * b, 128 * b + 128), V("es", 128 * b, 128 * b + 128), V("xq"), V("xs"))

    cp(V("nd16"), V("ndi"))
    act(V("rt"), ind(V("iK"), V("nd16")))
    for x in range(2):
        dma("y", T.nlf[:, 12 * x:12 * x + 12], T.rt[0:128:16, 192 * x:192 * x + 192], V("rt")[1], V("nlf", 12 * x, 12 * x + 12)[1])
    act(V("cap"), V("iC"), -1.0, F.Square, p16)
    act(V("cap"), V("cap"), -2.0 * BIG, bias=BIG)
    act(V("rs2"), V("iC"), 0.0, bias=BIG)
    cp(V("ul"), V("ui"))
    fill(V("rs2", 0, 384, 16), -BIG)
    quant(V("uq"), V("us"), V("ut"))
    run("v", lambda e: e.tensor_copy(T.urq[:, 0:128].bitcast(dt.uint32), T.uq[:, 0:128].bitcast(dt.uint32).indirect(T.ul[:, 0:8])),
        [V("uq"), V("ul")], [V("urq")], 250.0)
    act(V("urs"), ind(V("us"), V("ul")))
    score_products(V("urq"), V("urs"))
    act(V("ei"), ind(V("ari"), V("L4")))
    act(V("pw"), V("ei", 0, 576, 4))
    cp(V("nl"), V("nlf"))
    act(lm("lG"), lm("lC"), 12.0, bias=-12.0)
    act(lm("lD"), lm("lC"), -12.0, bias=276.0)
    ts(lm("lH"), lm("lC"), 7.0, A.is_ge, 1000.0, A.mult)
    tt(lm("lG"), lm("lG"), lm("lE"), A.add)
    tt(lm("lD"), lm("lD"), lm("lF"), A.add)
    tt(lm("lG"), lm("lG"), lm("lH"), A.add)
    ts(lm("lH"), lm("lC"), 0.0, A.is_equal, 289.0, A.mult)
    tt(lm("lG"), lm("lG"), lm("lD"), A.min)
    tt(lm("lG"), lm("lG"), lm("lI"), A.add)
    tt(lm("lG"), lm("lG"), lm("lH"), A.max)
    e0, e1 = lm("lF", 0, 23), lm("lF", 23, 46)
    act(lm("lA"), lm("lB"), 14.0, bias=314.0)
    act(lm("lC", 0, 23), lm("lB", 0, 23), 12.0, bias=290.0)
    ts(lm("lH"), lm("lF"), 12.0, A.is_ge, 288.0, A.mult)
    ts(lm("lI"), lm("lE"), 12.0, A.is_equal)
    tt(lm("lG"), lm("lG"), lm("lH"), A.max)
    tt(lm("lA"), lm("lA"), lm("lF"), A.add)
    tt(lm("lC", 0, 23), lm("lC", 0, 23), lm("lE", 0, 23), A.add)
    ts(lm("lD", 0, 23), e0, 13.0, A.is_equal)
    ts(lm("lD", 23, 46), e1, 13.0, A.is_lt)
    tt(lm("lA"), lm("lA"), lm("lI"), A.mult)
    tt(lm("lC", 0, 23), lm("lC", 0, 23), lm("lD", 0, 23), A.mult)
    tt(lm("lA", 23, 46), lm("lA", 23, 46), lm("lD", 23, 46), A.mult)
    tt(lm("lG", 0, 23), lm("lG", 0, 23), lm("lC", 0, 23), A.max)
    tt(lm("lG"), lm("lG"), lm("lA"), A.max)
    cp(V("L", 0, 23), lm("lG", 0, 23))
    cp(V("L", 24, 47), lm("lG", 23, 46))
    L0, L1 = V("L", 0, 23), V("L", 24, 47)

    def penalties():
        act(V("win2", 0, 144), V("pw"), PEN, F.Abs)
        act(V("win2", 144, 288), V("pw"), PEN, F.Abs)
        act(V("tp0"), ind(V("win2"), L0))

    def weights():
        act(V("win1", 0, 144), V("pw"), Q)
        act(V("win1", 144, 288), V("pw"), -Q)
        act(V("tb1"), ind(V("win1"), L1))

    def table_p():
        tt(V("pen"), ind(V("win2"), L1), V("tp0"), A.subtract)

    def table_b():
        tt(V("bt"), ind(V("win1"), L0), V("tb1"), A.subtract)

    for t in range(R):
        if t:
            score_products(V("urq"), V("urs"))
            unpack_products()
        for k in range(3):
            (cp if t else act)(V("psc", 128 * k, 128 * k + 128), V("psP", 512 * k, 512 * k + 128))

        def unpack(b):
            act(V("fh", CW * b, CW * b + 384), V("psE", 512 * b, 512 * b + 384), 0.5)

        def which(src, n, k):
            for x in range(2):
                end = n * x + n - 1
                act(V("junk", 16 * (k + x), 16 * (k + x) + n), V(src, n * x, end + 1), -1.0, F.Sign, V(src, end, end + 1), V("ix", k + x, k + x + 1))

        tt(V("gm"), ind(V("psc"), V("nl")), V("cap"), A.min)
        if t == 0:
            tt(V("win1", 290, 314), V("nlf"), V("k2i"), A.add)
            for x in range(2):
                act(V("win1", 314 + 14 * x, 326 + 14 * x), V("nlf", 12 * x, 12 * x + 12), bias=-4096.0)
                act(V("win1", 326 + 14 * x, 327 + 14 * x), p16, bias=384.0 + 16 * x - 4096.0)
            penalties()
            weights()
            table_p()
            table_b()
            for x in range(4):
                act(V("k2c", 13 * x, 13 * x + 12), V("win1", 290 + 12 * (x % 2), 302 + 12 * (x % 2)))
            for b in range(4):
                quant(V("eq", 128 * b, 128 * b + 128), V("es", 128 * b, 128 * b + 128), V("et", 3 - b, 515 - b))
            unpack_products()
        for b in range(4):
            unpack(b)
        scan(V("sc"), V("rs2"), V("gm"), -BIG, A.min, A.max)
        scan(V("pm1"), V("rs24"), V("sc", 15, 384, 16), -BIG, A.min, A.max)
        which("pm1", 12, 0)
        for x in range(2):
            cp(V("pen", 182 * x + 13, 182 * x + 13 + 155, 14), V("sc", 192 * x + 15, 192 * x + 192, 16))
        for x in range(2):
            ts(V("h1", 182 * x, 182 * x + 182), V("we"), V("ix", x, x + 1), A.is_gt)
        scan(V("s2"), V("h1"), V("pen", 0, 364), 0.0, A.mult, A.add)
        scan(V("pm2"), V("rs26"), V("s2", 13, 364, 14), -BIG, A.min, A.max)
        which("pm2", 13, 2)
        scan(V("kk", 0, 364), V("h1"), V("bt", 0, 364), 0.0, A.mult, A.add)
        for x in range(2):
            ts(V("h2", 182 * x, 182 * x + 182), V("we"), V("ix", 2 + x, 3 + x), A.is_gt)
        scan(V("kk", 364, 728), V("h2"), V("bt", 0, 364), 0.0, A.mult, A.add)
        tt(V("ka", 52, 104), V("k2c"), V("kk", 12, 728, 14), A.subtract)
        act(V("ka", 0, 52), V("kk", 13, 728, 14))
        ts(V("oK"), V("kk", 181, 728, 182), 4096.0, A.add)
        for b in range(4):
            act(V("sb", 3 * b + 1, 768, 12), ind(V("fh", CW * b, CW * b + CW), V("oK")), 2.0)
        scan(V("pmb", 1, 105), V("rsk"), V("ka"), -BIG, A.min, A.max)
        ts(V("di", 0, 8), V("pmb", 12, 105, 13), 384.0, A.max)
        tt(V("mn"), V("ka"), V("pmb", 0, 104), A.min)
        ts(V("dj", 0, 8), V("di", 0, 8), 511, A.bitwise_and)
        scan(V("sm"), V("rsk"), V("mn"), -BIG, A.min, A.max)
        cp(V("oA"), V("dj", 0, 8))
        for b in range(4):
            act(V("ga", 128 * b, 128 * b + 128), ind(V("fh", CW * b, CW * b + CW), V("oA")))
        ts(V("di", 8, 16), V("sm", 11, 104, 13), 384.0, A.max)
        ts(V("dj", 8, 16), V("di", 8, 16), 511, A.bitwise_and)
        cp(V("oB"), V("dj", 8, 16))
        for b in range(4):
            for k in range(2):
                tt(V("sa", 3 * b + k, 768, 12), ind(V("fh", CW * b, CW * b + CW), V("oB", 4 * k, 4 * k + 4)), V("ga", 128 * b + 64 * k, 128 * b + 64 * k + 64), A.add)
        scan(V("sy"), V("sa"), V("sb"), -BIG, A.max, A.subtract)
        cp(V("yt", 0, 256), V("sy", 1, 768, 3))
        quant(V("yc%d" % t), V("yp%d" % t), V("yt"))
        src, dst, ca, cb = route(T, topo, rank)
        sent = post([(dst if k is None else k, (out if k is None else mid) + str(t), mine + str(t), sem + str(t))
                     for k, sem, mid, out, mine in ((ca, "ac", "rc", "lc", "yc"), (cb, "ap", "rp", "lp", "yp"))])
        for f in range(2):
            for x in range(2):
                ts(V("oo", 26 * f + 13 * x, 26 * f + 13 * x + 13), V("it13"), V("ix", 2 * f + x, 2 * f + x + 1), A.is_equal, -2.0, A.mult)
        ts(V("pp"), V("kk", 12, 728, 14), -1.0 / Q, A.mult, 0.0, A.max)
        ts(V("nn"), V("kk", 12, 728, 14), 1.0 / Q, A.mult, 0.0, A.max)
        if t == 0:
            ts(V("pd", 3, 4), pt, 26.0, A.mult, p4, A.add)
            ts(V("pd", 4, 5), p1, -52.0, A.mult, 26.0, A.add)
            tt(V("uX"), V("uX"), V("uC"), A.add)
            ts(V("pd", 6, 7), pt, 26.0, A.mult, V("pd", 4, 5), A.add)
            ts(V("LI"), V("uY"), V("pd", 3, 4), A.add)
            ts(V("LJ"), V("uX"), V("pd", 6, 7), A.add)
        tt(V("w", 26, 78), V("pp"), V("oo"), A.add)
        for f in range(2):
            tt(V("w", 78 * f, 78 * f + 26), V("nn", 26 * f, 26 * f + 26), V("oo", 26 * f, 26 * f + 26), A.add)
        if t == 0:
            fill(V("sg"), -1.0)
            quant(V("zq"), V("zs"), V("zt"))
            fill(V("sg", 0, 576, 4), 0.0)
            fill(V("sg", 2, 576, 4), 1.0)
            for k in range(R):
                dma("y", u8(T, "lc%d" % k, 64, 128), u8(T, "zq", 64, 128), V("zq")[1], V("lc%d" % k, 64, 128)[1])
                dma("y", u8(T, "lp%d" % k, 64, 128), u8(T, "zs", 64, 128), V("zs")[1], V("lp%d" % k, 64, 128)[1])
        for b in range(4):
            act(V("y32", 64 * b, 64 * b + 64), V("yt", b, 256, 4), 32.0)
        half = ((0, 18), (18, 36))
        for a, b in half:
            act(V("ei", 16 * a, 16 * b), ind(V("w"), V("LI", a, b)))
        for b in range(4):
            act(V("fx", b, 1536, 4), V("fh", CW * b, CW * b + 384), 2.0)
        for b in range(4):
            ts(V("so", 4 * b, 4 * b + 4), V("kk", 181, 728, 182), 4.0, A.mult, 16384.0 + b, A.add)
        for a, b in half:
            tt(V("pr", 16 * a, 16 * b), ind(V("w"), V("LJ", a, b)), V("ei", 16 * a, 16 * b), A.mult)
        scan(V("s5"), V("sg"), V("pr"), 0.0, A.mult, A.add)
        tt(V("sp"), V("s5", 3, 576, 4), V("pw"), A.add)
        ts(V("pw"), V("sp"), -3.0, A.max, 3.0, A.min)
        if t < R - 1:
            penalties()
            weights()
            table_p()
            table_b()
        else:
            act(V("win1", 0, 144), V("pw"))
            act(V("win1", 144, 288), V("pw"), -1.0)
            act(V("tb1"), ind(V("win1"), L0))
            for x in range(2):
                for e in range(12):
                    act(V("ob", 144 * x + e, 144 * x + 144, 12), V("tb1", 182 * x + e, 182 * x + 168, 14))
            dma("y", T.oa[:], T.ob[:], V("ob")[1], [])
            quant(V("vq"), V("vs"), V("vt0"))
        sender, arr = route(T, topo, (rank - 1) % N), []
        for sem, k in (("ac%d" % t, sender[2]), ("ap%d" % t, sender[3])):
            arr.append((sem, len(topo.engines(sender[0] if k is None else k, core))))
        for b in range(4):
            mm(V("psE", 512 * b, 512 * b + 128), V("wq", 128 * b, 128 * b + 128), V("wp", 128 * b, 128 * b + 128), V("lc%d" % t), V("lp%d" % t), (sent, arr))
        for b in range(4):
            tt(V("vf", 64 * b, 64 * b + 64), V("psE", 512 * b, 512 * b + 64), V("y32", 64 * b, 64 * b + 64), A.add)
            ts(V("vt", 64 * b, 64 * b + 64), V("vf", 64 * b, 64 * b + 64), 0.03125, A.mult)
        run("v", lambda e: e.tensor_copy(T.fx[:, 0:1664].indirect(T.so[:, 0:16]), T.vt[:]), [V("vt"), V("so")], [V("fx")], 1000.0)

    score_products(V("vq"), V("vs"))
    dma("y", T.oc[:], u8(T, "xq", 0, 384), V("xq")[1], [])
    for k in range(4):
        dma("y", T.osc[4 * k:4 * k + 4, :], T.xs[32 * k:32 * k + 4, :], V("xs")[1], [])
    for k in range(3):
        cp(V("ysb", 128 * k, 128 * k + 128), V("psP", 512 * k, 512 * k + 128))
    dma("s", T.y[:], T.ysb[:], V("ysb")[1], [])
    issue()
    for sem in count:
        need("g", sem, count[sem], {})
